import numpy as np, ml_dtypes
CORES = [9,25,41,57]
N = 4
BF = ml_dtypes.bfloat16
W, NN, NL, P, C, ND, M, RO = 8192, 2048, 1024, 256, 64, 4, 4, 6
def look(E, wts, lim, q, D):
    u = (q @ wts) & 4095
    h = (u[:, 0] * u[:, 1]) >> 5
    slot = (h[:, None, None] + 613 * D[:, :, None] + np.arange(M)[None, None, :] * (2 * u[:, 0] + 1)[:, None, None]) & (W - 1)
    slot = slot.reshape(len(q), ND * M)
    dist = np.add.reduce(np.abs(E[slot] - q[:, None, :]), axis=2)
    ok = dist <= lim
    return np.where(np.any(ok, axis=1), slot[np.arange(len(q)), np.argmax(ok, axis=1)], -1), np.min(dist, axis=1)
def wish(NM, K, G):
    rho = np.add.reduce(G, axis=1) & 15
    return (NM[K[np.arange(len(K)), rho]] + G) & 255
def near(x, a, g):
    q = wish(x["NM"][a, g], x["L"][a, g][x["S"][a, g]], x["G"][a, g])
    return look(x["E"][a, g], x["WT"][a, g], 0, q, x["D"][a, g])[1]
def parts(rng):
    def w(hi, *shape): return rng.integers(0, hi, (N, 8) + shape, dtype=np.int32)
    return {"E": w(256, W, 16), "NM": w(256, NN, 16), "L": w(NN, NL, 16), "SG": w(NL, W), "DR": w(256, NL), "WT": w(256, 16, 2), "TH": 850 + w(350), "S": w(NL, P), "D": w(256, P, ND), "G": w(256, P, 16)}
def flat(v):
    return np.ascontiguousarray(v.transpose(0, 1, 3, 2)).reshape(N, 128, v.shape[2])
def tall(v):
    return np.ascontiguousarray(v.astype(np.float32).astype(np.int32).reshape(N, 8, 16, -1).transpose(0, 1, 3, 2))
def pack(x):
    def b(v): return flat(v).astype(np.float32).astype(BF)
    def i(v): return np.ascontiguousarray(v).astype(np.int32)
    return {"ent": b(x["E"]), "nm": b(x["NM"]), "lk": i(flat(x["L"])), "sg": i(x["SG"]), "dr": i(x["DR"]), "wt": i(x["WT"].reshape(N, 128, 2)), "th": i(np.repeat(x["TH"], 16, axis=1).reshape(N, 128, 1)),
            "s0": i(x["S"]), "d0": i(x["D"].transpose(0, 1, 3, 2).reshape(N, 8, ND * P)), "g0": b(x["G"])}
def setup_inputs(rng):
    return pack(parts(rng))
def setup_inputs_room(rng):
    x = parts(rng)
    for a in range(N):
        for g in range(8):
            v = near(x, a, g); lim = np.sort(v)[P // 2 - 1]; A = np.flatnonzero(v <= lim); B = np.flatnonzero(v > lim)
            x["TH"][a, g] = lim
            if len(B) == 0: continue
            n = int(rng.choice(np.array([0, 1, C - 1, C, C + 1, P])))
            if a == 0: n = (C, C + 1, P, C - 1, 1, 0, C, C + 1)[g]
            pick = rng.permutation(np.concatenate([rng.choice(A, P - n), rng.choice(B, n)]))
            for k in ("S", "D", "G"): x[k][a, g] = x[k][a, g][pick]
    return pack(x)
def setup_inputs_ties(rng):
    x = parts(rng)
    for k in ("E", "NM", "G"): x[k] = (x[k] >> 6) << 6
    x["TH"] = (64 * rng.integers(14, 18, (N, 8)) - (np.arange(8) & 1)[None, :]).astype(np.int32)
    r = N - 1
    x["TH"][r] = 4080; x["TH"][r, 5] = 2048; x["TH"][0, 5] = 4080
    for a in (r, 0): x["E"][a, 5] = x["E"][a, 5] & 64
    x["E"][r, 5, :, 0] = 0; x["NM"][r, 5] = 64; x["G"][r, 5] = x["G"][r, 5] & 64; x["G"][r, 5, ::2] = 128
    return pack(x)
def setup_inputs_alike(rng):
    x = parts(rng)
    for k in ("S", "D", "G"): x[k][:, 0] = x[k][:, 0, :1].copy()
    x["E"][:, 1] = x["E"][:, 1, :1].copy()
    x["SG"][:, 2] = rng.choice(np.array([0, NL - 1, 3]), (N, W))
    x["L"][:, 3] = rng.integers(0, NN, (N, 1, 1))
    x["D"][:, 4] = rng.integers(0, 256, (N, 1, 1))
    x["DR"][:, 5] = rng.integers(0, 256, (N, 1))
    x["WT"][:, 6] = 0
    x["E"][:, 7] = np.tile(x["E"][:, 7, :64].copy(), (1, W // 64, 1))
    return pack(x)
def setup_inputs_ends(rng):
    x = parts(rng); who = np.arange(N); even = who % 2 == 0; odd = ~even
    x["TH"][:, 0] = np.where(even, 4080, 0)
    x["NM"][odd, 0] = 0; x["G"][odd, 0, ::2] = 0; x["D"][odd, 0, ::4] = 0; x["L"][even, 0, ::2] = 0
    x["NM"][:, 1] = 0; x["TH"][:, 1] = 0; four = rng.integers(0, 256, (N, 4, 16))
    for a in range(N):
        x["E"][a, 1] = four[a][rng.integers(0, 4, W)]
        close = four[a].copy(); at = rng.integers(0, 16, 4); close[np.arange(4), at] = close[np.arange(4), at] ^ 1
        pool = np.concatenate([four[a], four[(a + 1) % N], close])
        x["G"][a, 1] = pool[rng.permutation(np.arange(P) % 12)]
    x["TH"][:, 2] = np.where(who == 0, 4080, np.where(who == 1, 4079, rng.integers(2000, 4079, N)))
    x["NM"][:, 2] = 0; x["E"][:, 2] = np.where(rng.random((N, W, 1)) < 0.5, 0, x["E"][:, 2]); x["G"][:, 2, ::2] = 255
    x["NM"][:, 3] = 0; x["WT"][:, 3] = 0; x["WT"][:, 3, 0] = 16; x["WT"][:, 3, 1] = 1; x["G"][:, 3, ::2, 0] = 255; x["G"][:, 3, ::2, 1] = 15
    x["L"][:, 4] = rng.choice(np.array([0, NN - 1]), (N, NL, 16)); x["SG"][:, 4] = rng.choice(np.array([0, NL - 1]), (N, W)); x["S"][:, 4] = rng.choice(np.array([0, NL - 1]), (N, P))
    x["DR"][:, 4] = rng.choice(np.array([0, 255]), (N, NL)); x["D"][:, 4] = rng.choice(np.array([0, 255]), (N, P, ND))
    for k in ("E", "NM", "G"): x[k][:, 5] = 255 * (x[k][:, 5] >> 7)
    x["TH"][:, 5] = 1529
    x["WT"][:, 6] = 255; x["NM"][:, 6] = 0; x["TH"][even, 6] = 4080
    x["G"][:, 6, ::2] = rng.integers(225, 256, (N, P // 2, 16)); x["G"][:, 6, 0] = 255
    x["TH"][:, 7] = 0
    return pack(x)
def setup_inputs_spread(rng):
    x = parts(rng)
    def col(n): return (np.exp2(rng.integers(0, 9, (N, 8, n, 1))) * rng.random((N, 8, n, 16))).astype(np.int32) * (rng.random((N, 8, n, 1)) > 0.0625)
    def low(hi, pw, *shape): return np.minimum((hi * rng.random((N, 8) + shape) ** pw).astype(np.int32), hi - 1)
    x["E"] = col(W); x["NM"] = col(NN); x["G"] = col(P)
    x["L"] = low(NN, 3, NL, 16); x["SG"] = low(NL, 2, W); x["DR"] = low(256, 2, NL); x["S"] = low(NL, 2, P); x["D"] = low(256, 3, P, ND)
    x["WT"] = np.minimum(np.exp2(8 * rng.random((N, 8, 16, 2))).astype(np.int32), 255)
    for a in range(N):
        for g in range(8):
            x["TH"][a, g] = np.sort(near(x, a, g))[int(rng.integers(P // 4, 3 * P // 4))]
    return pack(x)
def check_inputs(d):
    bad = []
    for k, hi in (("ent", 255), ("nm", 255), ("lk", NN - 1), ("sg", NL - 1), ("dr", 255), ("wt", 255), ("th", 4080), ("s0", NL - 1), ("d0", 255), ("g0", 255)):
        v = np.asarray(d[k]).astype(np.float64)
        if not (np.min(v) >= 0 and np.max(v) <= hi): bad.append("range of " + k)
        if np.any(v != np.floor(v)): bad.append("whole numbers in " + k)
    t = np.asarray(d["th"]).reshape(N, 8, 16)
    if np.any(t != t[:, :, :1]): bad.append("equal rows of a group in th")
    return bad
def reference(ent, nm, lk, sg, dr, wt, th, s0, d0, g0):
    E = tall(ent); NM = tall(nm); L = np.ascontiguousarray(lk.reshape(N, 8, 16, NL).transpose(0, 1, 3, 2)); WT = wt.astype(np.int32).reshape(N, 8, 16, 2)
    lim = th.reshape(N, 8, 16)[:, :, 0]
    G = tall(g0); D = np.array(d0.reshape(N, 8, ND, P).transpose(0, 1, 3, 2)).astype(np.int32)
    K = np.stack([np.stack([L[a, g][s0[a, g]] for g in range(8)]) for a in range(N)]).astype(np.int32)
    for step in range(RO):
        for a in range(N):
            b = (a + 1) % N
            for g in range(8):
                q = wish(NM[a, g], K[a, g], G[a, g])
                hit = look(E[a, g], WT[a, g], lim[a, g], q, D[a, g])[0]
                own = np.flatnonzero(hit >= 0); miss = np.flatnonzero(hit < 0)[:C]
                far = look(E[b, g], WT[b, g], lim[b, g], q[miss], D[a, g][miss])[0]
                G[a, g] = q
                for who, ix, slot in ((a, own, hit[own]), (b, miss[far >= 0], far[far >= 0])):
                    s = sg[who, g][slot]
                    G[a, g][ix] = E[who, g][slot]
                    K[a, g][ix] = L[who, g][s]
                    D[a, g][ix] = np.concatenate([dr[who, g][s][:, None], D[a, g][ix][:, :ND - 1]], axis=1)
    return {"yk": flat(K).astype(np.float32), "yd": np.ascontiguousarray(D.transpose(0, 1, 3, 2)).reshape(N, 8, ND * P).astype(np.float32), "yg": flat(G).astype(np.float32)}

@@ -1,0 +1,577 @@
+from concourse.mybir import dt, AluOpType, AxisListType, ActivationFunctionType
+
+A = AluOpType
+F = ActivationFunctionType
+STEPS = 6
+NC = 64
+KEEP, ASK, WIN = 8192, 8448, 8512
+BIGC = 23 * 262144
+SEL = 16384.0
+
+_sb = {
+    "EW": (WIN, "bfloat16"), "LKW": (WIN, "float32"), "LKP": (8192, "float32"), "NMW": (2048, "bfloat16"),
+    "LKI": (1024, "int32"), "LKD": (1024, "float32"), "SGI": (512, "int32"), "SGU": (512, "uint16"),
+    "WTI": (2, "int32"), "THI": (1, "int32"), "S0I": (256, "int32"), "S0H": (256, "float16"),
+    "DRI": (1024, "int32"), "DRT": (1024, "int32"), "DRL": (1024, "bfloat16"), "DRH": (1024, "bfloat16"),
+    "D32I": (256, "int32"), "D32T": (256, "int32"), "D32L": (256, "bfloat16"), "D32H": (256, "bfloat16"), "D32U": (256, "int32"),
+    "KI": (1, "int32"), "CI": (160, "int32"), "PI": (16, "int32"), "KT": (8, "int32"), "COL": (32, "float32"),
+    "RI": (160, "int32"), "R2": (160, "int32"), "W1F": (160, "float32"), "W2F": (160, "float32"), "SAME": (160, "float32"),
+    "C4": (160, "int32"), "C2": (160, "int32"), "C1": (160, "int32"), "CQ2": (160, "int32"), "CH": (128, "int32"),
+    "CK": (128, "int32"), "CKT": (128, "float32"), "CKU": (128, "float32"), "KEY": (128, "int32"), "CT": (128, "int32"), "CT2": (128, "int32"),
+    "CU": (128, "float32"), "CU2": (128, "float32"), "CU3": (128, "float32"), "CU4": (128, "float32"), "CU5": (128, "float32"), "CU6": (128, "float32"),
+    "SAM2": (128, "float32"), "E1": (128, "float32"), "EQ": (128, "float32"), "GT": (128, "float32"),
+    "GT1": (128, "float32"), "TC": (128, "float32"),
+    "SELB": (144, "bfloat16"), "BN": (144, "float16"), "BN8": (144, "float16"),
+    "BW1": (144, "bfloat16"), "BW2": (144, "bfloat16"), "BD": (576, "bfloat16"),
+    "TRIA": (128, "bfloat16"), "TRIB": (128, "bfloat16"), "TRIX": (128, "bfloat16"), "TRR": (128, "bfloat16"),
+    "IB": (128, "bfloat16"), "IM": (128, "bfloat16"), "I19": (128, "bfloat16"), "I8": (128, "bfloat16"), "IM8": (128, "bfloat16"),
+    "I256": (128, "float32"), "SHF": (128, "bfloat16"), "BO4": (128, "bfloat16"), "BO1": (128, "bfloat16"),
+    "BW1X": (128, "bfloat16"), "BW2X": (128, "bfloat16"), "RDX": (128, "bfloat16"), "QT": (128, "float32"),
+    "LO32": (128, "bfloat16"), "HI32": (128, "bfloat16"), "LO8": (128, "bfloat16"), "HI8": (128, "bfloat16"), "YDM": (32, "bfloat16"),
+    "MASK": (64, "float32"), "DIAG": (64, "float32"), "QOFF": (64, "uint16"),
+    "PD_": (16, "float32"), "CA": (16, "float32"), "CB": (16, "float32"), "CC": (16, "float32"), "CD": (4, "float32"),
+    "ZER": (16, "bfloat16"),
+    "GW": (320, "bfloat16"), "QW": (320, "int32"), "KW": (320, "int32"), "DW": (320, "bfloat16"),
+    "V": (256, "int32"), "DN": (256, "bfloat16"), "DB": (256, "bfloat16"),
+    "YI": (256, "int32"), "YA": (256, "int32"), "X": (256, "float16"), "QR": (256, "int32"),
+    "ND": (256, "int32"), "NDB": (256, "bfloat16"), "FBS": (256, "bfloat16"), "CM": (256, "bfloat16"),
+    "YI6": (64, "int32"), "YA6": (64, "int32"), "X6": (64, "float16"), "QR6": (64, "int32"),
+    "ND6": (64, "int32"), "NB6": (64, "bfloat16"), "FB6": (64, "bfloat16"), "CM6": (64, "bfloat16"), "RG": (64, "int32"),
+    "DC1": (64, "int32"), "DNC": (64, "bfloat16"), "DBC": (64, "bfloat16"),
+    "TM": (64, "float32"), "A1": (32, "float32"), "TN": (16, "float32"), "TN2": (16, "float32"), "LST": (16, "uint16"),
+    "LF": (16, "uint16"), "LO": (16, "uint16"), "LM": (16, "uint16"),
+    "Q4": (1024, "bfloat16"), "UI": (128, "int32"), "UM": (128, "int32"), "PR": (64, "int32"), "VV": (64, "int32"), "PV": (64, "int32"),
+    "SR": (256, "int32"), "SS": (256, "int32"), "OFF": (256, "uint16"), "NS": (256, "float32"),
+    "DA": (2048, "bfloat16"), "DD": (2048, "bfloat16"), "OK": (256, "bfloat16"), "MN": (256, "float32"), "AC": (256, "float32"),
+    "MS": (16, "bfloat16"), "CUM": (32, "bfloat16"), "OM": (16, "float32"), "FA": (16, "float32"), "FC": (16, "float32"),
+    "FB": (16, "float32"), "FD": (16, "float32"),
+    "PKS": (256, "float32"), "CQ": (512, "int32"), "QL": (64, "int32"), "RL": (64, "int32"), "RS": (64, "int32"),
+    "DQ": (64, "int32"), "DN1": (64, "int32"), "DNB": (64, "bfloat16"), "DK": (64, "int32"), "Q16": (1024, "bfloat16"),
+    "SA": (1024, "bfloat16"), "SD": (1024, "bfloat16"),
+    "G6": (64, "float32"), "SF": (4, "float32"), "TS": (4, "float32"), "LS": (4, "uint16"),
+    "OYK": (256, "float32"), "OYG": (256, "float32"), "OYD": (256, "float32"),
+}
+_ALONE = {"EW", "LKW", "LKP", "NMW", "LKI", "LKD", "SGI", "SGU", "GW", "CQ", "QL", "RL", "RS", "DA", "DD", "Q4", "Q16", "QW", "KW", "DW",
+          "WTI", "THI", "S0I", "DRI", "D32I", "OYK", "OYG", "OYD"}
+SCRATCH = {}
+PLACE = {}
+_top = {}
+for _n, (_w, _t) in _sb.items():
+    if _n in _ALONE:
+        SCRATCH["b" + _n] = ("sbuf", [128, _w], _t)
+        PLACE[_n] = ("b" + _n, 0)
+    else:
+        _p = "pool_" + _t
+        PLACE[_n] = (_p, _top.get(_p, 0))
+        _top[_p] = _top.get(_p, 0) + (_w + 31) // 32 * 32
+        SCRATCH[_p] = ("sbuf", [128, _top[_p]], _t)
+for _n in "ABCDEFGH":
+    SCRATCH["P" + _n] = ("psum", [128, 512], "float32")
+LOADS = ["ls0", "ldr", "ld0", "llk", "lnm", "lwt", "lth", "lg0", "lsg", "len"]
+SEMAPHORES = ["sv", "sp", "sa", "sg_", "qa", "ra", "ql", "rl", "o1", "o2", "o3"] + LOADS
+
+
+def rank_program(g, core, T, topo):
+    rank = T.rank_of(core)
+    if rank is None:
+        return
+    nxt = T.cores[(rank + 1) % len(T.cores)]
+    prv = T.cores[(rank - 1) % len(T.cores)]
+    eng = {"v": g.vector, "p": g.tensor, "a": g.scalar, "s": g.sync, "g": g}
+    own = {"v": "sv", "p": "sp", "a": "sa", "g": "sg_"}
+    cnt = {s: 0 for s in SEMAPHORES}
+    known = {e: {} for e in eng}
+    wr, rd = {}, {}
+    serial = [0]
+
+    def b(name, lo=None, hi=None, step=1, key=None, parts=128):
+        buf, at = PLACE[name] if name in PLACE else (name, 0)
+        w = _sb[name][0] if name in _sb else 512
+        lo = 0 if lo is None else lo
+        hi = w if hi is None else hi
+        last = at + lo + ((hi - lo - 1) // step) * step + 1
+        keys = key if isinstance(key, tuple) else (key or name,)
+        return (keys, T[buf][0:parts, at + lo:last:step] if step > 1 else T[buf][0:parts, at + lo:at + hi])
+
+    def ind(win, off):
+        return (win[0] + off[0], win[1].indirect(off[1]))
+
+    def need(e, R, W):
+        toks = []
+        for k in R:
+            toks += [(t, True) for t in wr.get(k, [])]
+            if len(k) == 2 and k[0] == "P" and k[1] in "ABCDEFGH":
+                toks += [(t, False) for t in rd.get(k, [])]
+        for k in W:
+            toks += [(t, False) for t in wr.get(k, []) + rd.get(k, [])]
+        toks.sort(key=lambda x: -x[0][3])
+        for (s, n, clk, _i, te), raw in toks:
+            if te == e == "p" and not raw:
+                continue
+            if known[e].get(s, 0) >= n:
+                continue
+            eng[e].wait_ge(T.sem[s], n)
+            for s2, n2 in clk.items():
+                if known[e].get(s2, 0) < n2:
+                    known[e][s2] = n2
+            known[e][s] = n
+
+    def note(e, s, R, W, te):
+        serial[0] += 1
+        clk = dict(known[e])
+        clk[s] = cnt[s]
+        tok = (s, cnt[s], clk, serial[0], te)
+        for k in R:
+            rd.setdefault(k, []).append(tok)
+        for k in W:
+            wr[k] = [tok]
+            rd[k] = []
+
+    def split(args, R):
+        out = []
+        for x in args:
+            if isinstance(x, tuple):
+                R.extend(x[0])
+                out.append(x[1])
+            else:
+                out.append(x)
+        return out
+
+    def op(e, meth, out, *args, sem=None, inc=1, W=None, **kw):
+        R = []
+        a = split(args, R)
+        kv = {k: split([v], R)[0] for k, v in kw.items()}
+        w = W or list(out[0])
+        R.extend(k for k in out[0] if k not in w)
+        need(e, R, w)
+        f = {"v": {"tt": eng["v"].tensor_tensor, "ts": eng["v"].tensor_scalar, "cp": eng["v"].tensor_copy, "red": eng["v"].tensor_reduce,
+                   "scan": eng["v"].tensor_tensor_scan, "set": eng["v"].memset},
+             "a": {"act": eng["a"].activation, "dma": eng["a"].dma_start}, "s": {"dma": eng["s"].dma_start},
+             "g": {"iota": g.iota}}[e][meth]
+        s = sem or own[e]
+        f(out[1], *a, **kv).then_inc(T.sem[s], inc)
+        cnt[s] += inc
+        note(e, s, R, w, e if sem is None else s)
+
+    def mm(out, parts):
+        R = []
+        for j, x in enumerate(parts):
+            r = []
+            l = split(list(x), r)
+            need("p", r, list(out[0]) if j == 0 else [])
+            R += r
+            i = eng["p"].matmul(out[1], l[0], l[1], j == 0, j == len(parts) - 1)
+        i.then_inc(T.sem["sp"], 1)
+        cnt["sp"] += 1
+        note("p", "sp", R, list(out[0]), "p")
+
+    def ts(out, x, s1, o1, s2=None, o2=None):
+        if o2 is None:
+            op("v", "ts", out, x, s1, None, o1)
+        else:
+            op("v", "ts", out, x, s1, s2, o1, o2)
+
+    def tt(out, x, y, o):
+        op("v", "tt", out, x, y, o)
+
+    def cp(out, x):
+        op("v", "cp", out, x)
+
+    def act(out, x, f=F.Copy, **kw):
+        op("a", "act", out, x, f, **kw)
+
+    def load(q, sem, out, src):
+        op(q, "dma", out, src, sem=sem, inc=16)
+
+    def send(dst, land, src, rsem, lsem):
+        need("g", list(src[0]), [])
+        rid, pid = topo.addr(dst)[0:2]
+        g.remote_dma(land[1], src[1], T.sem[rsem], T.sem[lsem], pid, rid, topo.mask(core, dst))
+        cnt[lsem] += len(topo.engines(core, dst))
+        note("g", lsem, list(src[0]), [], lsem)
+
+    def arrive(key, sem, src):
+        cnt[sem] += len(topo.engines(src, core))
+        serial[0] += 1
+        wr[key] = [(sem, cnt[sem], {sem: cnt[sem]}, serial[0], sem)]
+        rd[key] = []
+
+    def col(j):
+        return b("COL", j, j + 1, key="COL%d" % j)
+
+    def kt(j):
+        return b("KT", j, j + 1, key="KT%d" % j)
+
+    load("a", "ldr", b("DRI", parts=8), T.dr[:])
+    load("s", "ls0", b("S0I", parts=8), T.s0[:])
+    load("a", "llk", b("LKI"), T.lk[:])
+    load("s", "lwt", b("WTI"), T.wt[:])
+    load("s", "lsg", b("SGI"), T.sg[:])
+    load("s", "lg0", b("GW", 64, 320, key="G"), T.g0[:])
+    load("s", "ld0", b("D32I", parts=32), T.d0[:])
+    load("s", "lth", b("THI"), T.th[:])
+    load("s", "lnm", b("NMW"), T.nm[:])
+    load("s", "len", b("EW", 0, KEEP, key="EW.e"), T.ent[:])
+
+    for nm, pattern, down in (("KI", [[0, 1]], 1), ("C4", [[1, 10], [0, 16]], 0), ("CT", [[0, 16], [1, 8]], 0), ("C1", [[0, 40], [1, 4]], 0),
+                              ("CI", [[1, 160]], 0), ("CQ2", [[0, 10], [1, 4], [0, 4]], 0), ("KEY", [[4, 8], [0, 4], [1, 4]], 0),
+                              ("CK", [[1, 128]], -1), ("C2", [[1, 40], [0, 4]], 0), ("CT2", [[0, 8], [1, 16]], 0), ("PI", [[16, 16]], 1)):
+        op("g", "iota", b(nm), pattern, 0, down)
+    SAME = b("SAME", 0, 128)
+    ts(kt(0), b("KI"), 4, A.arith_shift_right)
+    ts(kt(4), b("KI"), 2, A.arith_shift_right, 3, A.bitwise_and)
+    cp(col(4), b("KI"))
+    ts(col(0), kt(0), 16.0, A.mult)
+    cp(col(1), kt(0))
+    cp(col(17), kt(4))
+    ts(b("CKT"), b("C4", 0, 128), col(4), A.is_equal, 128.0, A.mult)
+    ts(b("CU"), b("CT"), 0.0, A.is_equal, 16.0, A.mult)
+    ts(b("CU2"), b("CT"), 4.0, A.is_equal)
+    tt(b("CU3"), b("CU"), b("CU2"), A.subtract)
+    tt(b("HI8"), b("CKT"), b("CU2"), A.mult)
+    tt(b("LO8"), b("CKT"), b("CU3"), A.mult)
+    ts(b("DRT", parts=8), b("DRI", parts=8), 15, A.bitwise_and)
+    cp(b("DRH", parts=8), b("DRI", parts=8))
+    cp(b("DRL", parts=8), b("DRT", parts=8))
+    for h, pb in ((0, "PD"), (1, "PE")):
+        mm(b(pb), [(b("HI8", parts=8), b("DRH", 512 * h, 512 * h + 512, parts=8)), (b("LO8", parts=8), b("DRL", 512 * h, 512 * h + 512, parts=8))])
+    cp(b("SGU"), b("SGI"))
+    for h, pb in ((0, "PD"), (1, "PE")):
+        tt(b("LKD", 512 * h, 512 * h + 512), b("LKI", 512 * h, 512 * h + 512), b(pb), A.add)
+    for h in range(2):
+        act(b("LKP", 4096 * h, 4096 * h + 4096, key="LKP%d" % h), ind(b("LKD"), b("SGU", 256 * h, 256 * h + 256)), F.Identity, bias=32768.0)
+
+    ts(b("W1F"), b("C4"), col(4), A.is_equal)
+    ts(b("W2F"), b("C1"), 3.0, A.is_equal)
+    ts(b("SAME", key="SAME"), b("C4"), col(1), A.is_equal)
+    tt(b("BN8"), b("W1F", 0, 144), b("W2F", 0, 144), A.mult)
+    tt(b("BN"), b("SAME", 0, 144), b("W2F", 0, 144), A.mult)
+    ts(b("MASK"), b("C1", 0, 64), col(17), A.is_equal)
+    cp(b("S0H", parts=8), b("S0I", parts=8))
+    mm(b("PA", 256, 320), [(b("BN8", 3 - y, 131 - y, parts=8), b("S0H", y, 256, 4, parts=8)) for y in range(4)])
+    ts(b("BO4"), SAME, 4096.0, A.mult)
+    ts(kt(2), b("KI"), 15, A.bitwise_and)
+    ts(kt(3), b("KI"), 3, A.bitwise_and)
+    ts(kt(5), kt(2), -1.0, A.mult)
+    ts(kt(6), kt(5), 15, A.bitwise_and)
+    ts(col(5), kt(6), 4096.0, A.mult)
+
+    Gm = b("GW", 64, 320, key="G")
+    Km = b("KW", 64, 320, key="KW1")
+    Qm = b("QW", 64, 320, key="QW1")
+    q = b("EW", KEEP, ASK, key="EW.q")
+    oldk = b("LKW", KEEP, ASK, key="LKW.k")
+    ENT = b("EW", 0, KEEP, key="EW.e")
+    EALL = b("EW", key=("EW.e", "EW.q", "EW.s"))
+    LALL = b("LKW", key=("LKW.e", "LKW.k", "LKW.s"))
+
+    def dense(ps, n, out):
+        tt(b("TM", 0, n), ps, b("MASK", 0, n), A.mult)
+        tt(b("A1", 0, n // 2), b("TM", 0, n, 2), b("TM", 1, n, 2), A.add)
+        tt(out, b("A1", 0, n // 2, 2), b("A1", 1, n // 2, 2), A.add)
+
+    def rho_sums(gs, n):
+        mm(b("PA", 0, n), [(b("BO4"), gs)])
+
+    def chosen_link(ks, n, x):
+        yi, ya, xx = b("YI" + x, 0, n), b("YA" + x, 0, n), b("X" + x, 0, n)
+        ts(yi, b("PA", 0, n), col(5), A.add)
+        ts(ya, yi, 61440, A.bitwise_and)
+        tt(xx, ya, ks, A.max)
+        mm(b("PA", 256, 256 + n // 4), [(b("BN", 3 - y, 131 - y), b("X" + x, y, n, 4)) for y in range(4)])
+
+    def wish(gs, n, x, out):
+        dense(b("PA", 256, 256 + n // 4), n // 4, b("TN2", 0, n // 16))
+        ts(b("LST", 0, n // 16), b("TN2", 0, n // 16), -491520.0, A.add)
+        tt(b("QR" + x, 0, n), ind(b("NMW"), b("LST", 0, n // 16)), gs, A.add)
+        ts(out, b("QR" + x, 0, n), 255, A.bitwise_and)
+
+    dense(b("PA", 256, 320), 64, b("TN"))
+    cp(b("LST"), b("TN"))
+    cp(Km, ind(b("LKI"), b("LST")))
+    rho_sums(Gm, 256)
+    chosen_link(Km, 256, "")
+    cp(oldk, Km)
+    ts(b("CKU"), b("KEY"), col(4), A.is_equal)
+    ts(b("CH"), b("CQ2", 0, 128), 1, A.bitwise_and)
+    ts(b("CU4"), b("CH"), 0.0, A.is_equal)
+    tt(b("LO32"), b("CKU"), b("CU4"), A.mult)
+    tt(b("HI32"), b("CKU"), b("CH"), A.mult)
+    ts(b("D32T", parts=32), b("D32I", parts=32), 15, A.bitwise_and)
+    ts(b("D32U", parts=32), b("D32I", parts=32), 4, A.arith_shift_right)
+    cp(b("D32L", parts=32), b("D32T", parts=32))
+    cp(b("D32H", parts=32), b("D32U", parts=32))
+    mm(b("PH", 0, 256), [(b("LO32", parts=32), b("D32L", parts=32)), (b("HI32", parts=32), b("D32H", parts=32))])
+    wish(Gm, 256, "", Qm)
+    cp(q, Qm)
+    cp(b("COL", 20, 22, key="COLW"), b("WTI"))
+    cp(b("COL", 22, 23, key="COL22"), b("THI"))
+    th = b("COL", 22, 23, key="COL22")
+    w1c, w2c = b("COL", 20, 21, key="COLW"), b("COL", 21, 22, key="COLW")
+    ts(b("RI"), b("CI"), col(0), A.subtract)
+    ts(b("R2"), b("RI"), 2, A.arith_shift_right)
+    cp(b("DN"), b("PH", 0, 256))
+    ts(b("BW1"), b("R2", 0, 144), 3.0, A.is_equal, w1c, A.mult)
+    ts(b("BW2"), b("R2", 0, 144), 3.0, A.is_equal, w2c, A.mult)
+    ts(col(6), kt(3), 64.0, A.mult)
+    ts(col(7), kt(3), 32.0, A.mult, float(-BIGC), A.add)
+    for j, w in enumerate((612.0 * 32, 9792.0 * 32, 32.0, 512.0)):
+        ts(col(24 + j), kt(4), float(j), A.is_equal, w, A.mult)
+    tt(col(28), col(24), col(25), A.add)
+    tt(col(29), col(26), col(27), A.add)
+    tt(col(8), col(28), col(29), A.add)
+    for d in range(4):
+        ts(col(10 + d), kt(3), float(d), A.is_equal, col(8), A.mult)
+    for d in range(4):
+        ts(b("BD", 144 * d, 144 * d + 144, key="BD%d" % d), b("R2", 0, 144), 3.0, A.is_equal, col(10 + d), A.mult)
+    act(b("DB"), b("DN"), F.Identity, bias=8.0)
+    op("v", "set", b("COL", 30, 31, key="COL30"), -15.5)
+    op("v", "set", b("COL", 31, 32, key="COL31"), -16.0)
+
+    def rest_of_constants():
+        ts(b("SELB"), b("RI", 0, 144), 15.0, A.is_equal)
+        ts(kt(1), b("KI"), 2, A.arith_shift_right)
+        ts(b("E1"), b("CK"), 0.0, A.is_equal)
+        ts(b("EQ"), b("CK"), 0.0, A.is_equal, SEL, A.mult)
+        ts(b("GT"), b("CK"), 0.0, A.is_gt, SEL, A.mult)
+        cp(col(2), kt(1))
+        cp(col(3), kt(2))
+        cp(col(9), kt(3))
+        ts(b("SAM2"), b("C2", 0, 128), col(2), A.is_equal)
+        tt(b("TC"), b("EQ"), b("GT"), A.subtract)
+        ts(b("QT"), b("KEY"), col(2), A.is_equal)
+        for nm, w in (("IB", 1.0), ("I19", 524288.0), ("I256", 256.0), ("IM", -4096.0), ("I8", 8.0), ("IM8", -8.0)):
+            act(b(nm), b("E1"), scale=w)
+        act(b("TRIB"), b("SAM2"), scale=-SEL)
+        for nm, w in (("BO1", 1.0), ("BW1X", w1c), ("BW2X", w2c)):
+            act(b(nm), SAME, scale=w)
+        tt(b("TRIA"), b("SAM2"), b("TC"), A.mult)
+        tt(b("TRIX"), SAME, b("TC"), A.mult)
+        ts(b("CU5"), b("CK"), 0.0, A.is_ge)
+        tt(b("TRR"), SAME, b("CU5"), A.mult)
+        ts(b("CU4"), b("CQ2", 0, 128), col(9), A.is_equal, col(8), A.mult)
+        tt(b("RDX"), b("CU4"), SAME, A.mult)
+        ts(b("GT1"), b("CK"), 1.0, A.is_equal)
+        ts(b("CU6"), b("C1", 0, 128), 0.0, A.not_equal)
+        tt(b("SHF"), b("GT1"), b("CU6"), A.mult)
+        ts(b("DIAG"), b("CT2", 0, 64), col(3), A.is_equal)
+        cp(b("QOFF"), b("CI", 0, 64))
+        ts(b("PD_"), b("PI"), col(0), A.subtract)
+        ts(b("CA"), b("PD_"), 256.0 - 4095.0, A.add)
+        ts(b("CB"), b("PD_"), 64.0 - 4095.0, A.add)
+        ts(b("CC"), b("PD_"), -1.0, A.mult, SEL - KEEP, A.add)
+        ts(b("CD"), b("PD_", 0, 4), -1.0, A.mult, SEL - ASK, A.add)
+        op("v", "set", b("ZER"), 0.0)
+        op("v", "set", b("CUM"), 0.0)
+        op("v", "set", b("CQ"), 0)
+        op("v", "set", b("EW", ASK, WIN, key="EW.s"), 0.0)
+        op("v", "set", b("LKW", ASK, WIN, key="LKW.s"), 0.0)
+        ts(col(14), kt(4), 0.0, A.is_equal)
+        ts(col(15), kt(4), 1.0, A.is_equal, 16.0, A.mult)
+        ts(col(19), col(1), 4.0, A.mult)
+        tt(col(18), col(14), col(15), A.add)
+        tt(col(23), col(19), col(9), A.add)
+        ts(b("YDM"), b("CI", 0, 32), col(23), A.is_equal, col(18), A.mult)
+
+    def nibbles(v, n, x):
+        ts(b("ND" + x, 0, n), v, 11, A.arith_shift_right, 31, A.bitwise_and)
+        nb = b("NDB" if n == 256 else "NB6")
+        fb = b("FBS" if n == 256 else "FB6")
+        cp(nb, b("ND" + x, 0, n))
+        act(fb, nb, F.Sign, bias=b("COL", 30, 31, key="COL30"))
+        return nb, fb
+
+    def directories(nb, fb, n, dn, db, cm, out):
+        mm(b("PH", 256, 256 + n), [(b("SHF"), dn), (b("IB"), nb), (b("I8"), fb)])
+        tt(cm, b("PH", 256, 256 + n), db, A.max)
+        mm(b("PH", 0, n), [(b("IB"), cm), (b("IM8"), fb)])
+        act(out, b("PH", 0, n), F.Identity, bias=b("COL", 31, 32, key="COL31"))
+
+    for step in range(STEPS):
+        last = step == STEPS - 1
+        mm(b("PB", 0, 64), [(b("BW1", 12 - 4 * y, 140 - 4 * y), b("EW", KEEP + y, ASK, 4, key="EW.q")) for y in range(4)])
+        mm(b("PB", 64, 128), [(b("BW2", 12 - 4 * y, 140 - 4 * y), b("EW", KEEP + y, ASK, 4, key="EW.q")) for y in range(4)])
+        for d in range(4):
+            mm(b("PC", 64 * d, 64 * d + 64), [(b("BD", 144 * d + 12 - 4 * y, 144 * d + 140 - 4 * y, key="BD%d" % d), b("DN", y, 256, 4)) for y in range(4)])
+        for m in range(4):
+            act(b("Q4", m, 1024, 4), q)
+        if step == 0:
+            rest_of_constants()
+        cp(b("UI"), b("PB", 0, 128))
+        ts(b("UM"), b("UI"), 4095, A.bitwise_and)
+        tt(b("PR"), b("UM", 0, 64), b("UM", 64, 128), A.mult)
+        ts(b("VV"), b("UM", 0, 64), col(6), A.mult, col(7), A.add)
+        tt(b("PV"), b("PR"), b("VV"), A.add)
+
+        def probes(d0, d1):
+            k0, k1 = 64 * d0, 64 * d1
+            for d in range(d0, d1):
+                tt(b("SR", 64 * d, 64 * d + 64, key="SR.%d" % d), b("PV"), b("PC", 64 * d, 64 * d + 64), A.add)
+            ts(b("SS", k0, k1, key="SS%d" % d0), b("SR", k0, k1, key=tuple("SR.%d" % d for d in range(d0, d1))), 5, A.arith_shift_right, 8191, A.bitwise_and)
+            cp(b("OFF", k0, k1, key="OFF%d" % d0), b("SS", k0, k1, key="SS%d" % d0))
+
+        def probe(d, h):
+            lo = 1024 * (d % 2) + 512 * h
+            k = "%d.%d" % (d % 2, h)
+            tt(b("DA", lo, lo + 512, key="DA" + k), ind(ENT, b("OFF", 64 * d + 32 * h, 64 * d + 32 * h + 32, key="OFF%d" % (1 if d else 0))),
+               b("Q4", 512 * h, 512 * h + 512), A.subtract)
+            act(b("DD", lo, lo + 512, key="DD" + k), b("DA", lo, lo + 512, key="DA" + k), F.Abs)
+
+        def distance(d):
+            x = d % 2
+            ks = ("DD%d.0" % x, "DD%d.1" % x)
+            mm(b("PD" if x == 0 else "PE", 0, 64), [(b("SELB", 15 - z, 143 - z), b("DD", 1024 * x + z, 1024 * x + 1024, 16, key=ks)) for z in range(16)])
+
+        def okay(d):
+            ts(b("OK", 64 * d, 64 * d + 64, key="OK%d" % d), b("PD" if d % 2 == 0 else "PE", 0, 64), th, A.is_le)
+            mm(b("PF" if d % 2 == 0 else "PG", 0, 64),
+               [(b("TRIB"), b("OK", 64 * e, 64 * e + 64, key="OK%d" % e)) for e in range(d)] + [(b("TRIA"), b("OK", 64 * d, 64 * d + 64, key="OK%d" % d))])
+
+        def first(d):
+            mn = b("MN", 64 * d, 64 * d + 64, key="MN%d" % d)
+            tt(mn, b("PF" if d % 2 == 0 else "PG", 0, 64), b("NS", 64 * d, 64 * d + 64, key="NS%d" % (1 if d else 0)), A.min)
+            ac = b("AC", 64 * d, 64 * d + 64, key="AC%d" % d)
+            if d == 0:
+                ts(ac, mn, 0.0, A.max)
+            else:
+                tt(ac, mn, b("AC", 64 * d - 64, 64 * d, key="AC%d" % (d - 1)), A.max)
+
+        probes(0, 1)
+        probe(0, 0)
+        probe(0, 1)
+        probes(1, 4)
+        mm(b("PH", 0, 256), [(b("I256"), oldk), (b("I19"), b("DN")), (b("IB"), q)])
+        distance(0)
+        probe(1, 0)
+        probe(1, 1)
+        distance(1)
+        act(b("PKS"), b("PH", 0, 256))
+        probe(2, 0)
+        probe(2, 1)
+        okay(0)
+        distance(2)
+        probe(3, 0)
+        okay(1)
+        probe(3, 1)
+        ts(b("NS", 0, 64, key="NS0"), b("SS", 0, 64, key="SS0"), -1.0, A.mult, SEL, A.add)
+        first(0)
+        okay(2)
+        ts(b("NS", 64, 256, key="NS1"), b("SS", 64, 256, key="SS1"), -1.0, A.mult, SEL, A.add)
+        distance(3)
+        first(1)
+        first(2)
+        okay(3)
+        first(3)
+        mm(b("PF", 64, 128), [(b("QT"), b("AC", 192, 256, key="AC3"))])
+        dense(b("PF", 64, 128), 64, b("TN"))
+        ts(b("MS"), b("TN"), 0.0, A.is_equal)
+        op("v", "scan", b("CUM", 1, 17), b("MS"), b("ZER"), 0.0, A.add, A.add)
+        mm(b("PG", 64, 80), [(b("TRR"), b("MS")), (b("IM"), b("MS")), (b("BO1"), b("CUM", 0, 16))])
+        tt(b("OM"), b("PG", 64, 80), b("CA"), A.min)
+        ts(b("LO"), b("OM"), 4095.0, A.add)
+        op("v", "cp", (("CQ", "LO"), b("CQ")[1].indirect(b("LO")[1])), b("PKS"), W=["CQ"])
+        send(nxt, b("QL"), b("CQ", 0, NC), "qa", "ql")
+        if step == 0:
+            for z in range(16):
+                act(b("LKW", 512 * z, 512 * z + 512, key="LKW.e"), b("LKP", z, 8192, 16, key=("LKP0", "LKP1")))
+
+        tt(b("FC"), b("TN"), b("CC"), A.max)
+        ts(b("LF"), b("FC"), -1.0, A.mult, SEL, A.add)
+
+        def next_state():
+            act(Gm, ind(EALL, b("LF")))
+            if not last:
+                rho_sums(Gm, 256)
+            cp(b("V"), ind(LALL, b("LF")))
+            ts(Km, b("V"), 2047, A.bitwise_and)
+            if not last:
+                chosen_link(Km, 256, "")
+            return nibbles(b("V"), 256, "")
+
+        if step:
+            nb, fb = next_state()
+
+        arrive("QL", "qa", prv)
+        sq = b("EW", ASK, WIN, key="EW.s")
+        ts(b("DQ"), b("QL"), 255, A.bitwise_and)
+        cp(sq, b("DQ"))
+        for h in range(2):
+            act(b("Q16", 512 * h, 512 * h + 512, key="Q16%d" % h), ind(sq, b("QOFF", 32 * h, 32 * h + 32)), F.Copy)
+        mm(b("PB", 128, 192), [(b("BW1X"), sq)])
+        mm(b("PB", 192, 256), [(b("BW2X"), sq)])
+        ts(b("DN1"), b("QL"), 19, A.arith_shift_right)
+        cp(b("DNB"), b("DN1"))
+        mm(b("PC", 0, 64), [(b("RDX"), b("DNB"))])
+        cp(b("UI"), b("PB", 128, 256))
+        ts(b("UM"), b("UI"), 4095, A.bitwise_and)
+        tt(b("PR"), b("UM", 0, 64), b("UM", 64, 128), A.mult)
+        ts(b("VV"), b("UM", 0, 64), col(6), A.mult, col(7), A.add)
+        tt(b("PV"), b("VV"), b("PC", 0, 64), A.add)
+        tt(b("SR", 0, 64, key="SR.0"), b("PR"), b("PV"), A.add)
+        ts(b("SS", 0, 64, key="SS0"), b("SR", 0, 64, key="SR.0"), 5, A.arith_shift_right, 8191, A.bitwise_and)
+        cp(b("OFF", 0, 64, key="OFF0"), b("SS", 0, 64, key="SS0"))
+        for c in range(4):
+            sa, sd = b("SA", 256 * c, 256 * c + 256, key="SA%d" % c), b("SD", 256 * c, 256 * c + 256, key="SD%d" % c)
+            tt(sa, ind(ENT, b("OFF", 16 * c, 16 * c + 16, key="OFF0")), b("Q16", 256 * c, 256 * c + 256, key="Q16%d" % (c // 2)), A.subtract)
+            act(sd, sa, F.Abs)
+        ts(b("DK"), b("QL"), 8, A.arith_shift_right, 2047, A.bitwise_and)
+        cp(b("LKW", ASK, WIN, key="LKW.s"), b("DK"))
+        ts(b("NS", 0, 64, key="NS0"), b("SS", 0, 64, key="SS0"), -1.0, A.mult, SEL, A.add)
+        ts(b("FA"), b("OM"), 63.5 - 4095.0, A.is_gt, SEL, A.mult)
+        tt(b("FD"), b("OM"), b("FA"), A.add)
+        tt(b("FB"), b("FD"), b("CB"), A.min)
+        ts(b("LM"), b("FB"), 4095.0, A.add)
+        mm(b("PD", 0, 64), [(b("SELB", 15 - x, 143 - x), b("SD", x, 1024, 16, key=("SD0", "SD1", "SD2", "SD3"))) for x in range(16)])
+        ts(b("OK", 0, 64, key="OK0"), b("PD", 0, 64), th, A.is_le)
+        mm(b("PF", 0, 64), [(b("TRIX"), b("OK", 0, 64, key="OK0"))])
+        tt(b("MN", 0, 64, key="MN0"), b("PF", 0, 64), b("NS", 0, 64, key="NS0"), A.min)
+        ts(b("AC", 0, 64, key="AC0"), b("MN", 0, 64, key="MN0"), 0.0, A.max)
+        mm(b("PG", 0, 64), [(SAME, b("AC", 0, 64, key="AC0"))])
+        tt(b("TM"), b("PG", 0, 64), b("DIAG"), A.mult)
+        for c in range(4):
+            op("v", "red", b("TS", c, c + 1), b("TM", 16 * c, 16 * c + 16), AxisListType.X, A.add)
+        tt(b("SF"), b("TS"), b("CD"), A.max)
+        ts(b("LS"), b("SF"), -1.0, A.mult, SEL, A.add)
+        ts(b("G6"), ind(EALL, b("LS")), 65536.0, A.mult)
+        tt(b("RS"), ind(LALL, b("LS")), b("G6"), A.add)
+        send(prv, b("RL"), b("RS"), "ra", "rl")
+
+        if step == 0:
+            nb, fb = next_state()
+        if not last:
+            wish(Gm, 256, "", Qm)
+        directories(nb, fb, 256, b("DN"), b("DB"), b("CM"), b("DW", 64, 320, key="DW1"))
+        ts(b("DC1"), b("CQ", 0, NC), 19, A.arith_shift_right)
+        cp(b("DNC"), b("DC1"))
+        ts(b("DBC"), b("DC1"), 8.0, A.add)
+
+        arrive("RL", "ra", nxt)
+        g6 = b("GW", 0, 64, key="GR")
+        k6 = b("KW", 0, 64, key="KW0")
+        ts(b("RG"), b("RL"), 16, A.arith_shift_right)
+        ts(k6, b("RL"), 2047, A.bitwise_and)
+        cp(g6, b("RG"))
+        if not last:
+            rho_sums(g6, 64)
+        nb, fb = nibbles(b("RL"), 64, "6")
+        if not last:
+            chosen_link(k6, 64, "6")
+        directories(nb, fb, 64, b("DNC"), b("DBC"), b("CM6"), b("DW", 0, 64, key="DW0"))
+        act(b("DN"), ind(b("DW", key=("DW0", "DW1")), b("LM")))
+        if not last:
+            act(b("DB"), b("DN"), F.Identity, bias=8.0)
+            wish(g6, 64, "6", b("QW", 0, 64, key="QW0"))
+            cp(q, ind(b("QW", key=("QW0", "QW1")), b("LM")))
+            cp(oldk, ind(b("KW", key=("KW0", "KW1")), b("LM")))
+
+    cp(b("OYG"), ind(b("GW", key=("GR", "G")), b("LM")))
+    op("s", "dma", (("yg",), T.yg[:]), b("OYG"), sem="o1", inc=16)
+    cp(b("OYK"), ind(b("KW", key=("KW0", "KW1")), b("LM")))
+    op("s", "dma", (("yk",), T.yk[:]), b("OYK"), sem="o2", inc=16)
+    mm((("PA",), T.PA[0:32, 0:256]), [(b("YDM"), b("DN"))])
+    cp(b("OYD", parts=32), (("PA",), T.PA[0:32, 0:256]))
+    op("s", "dma", (("yd",), T.yd[:]), b("OYD", parts=32), sem="o3", inc=16)
+    for s in SEMAPHORES:
+        if cnt[s] > known["g"].get(s, 0):
+            g.wait_ge(T.sem[s], cnt[s])
+            known["g"][s] = cnt[s]

@@ -7,6 +7,7 @@ NC = 64
 KEEP, ASK, WIN = 8192, 8448, 8512
 BIGC = 23 * 262144
 SEL = 16384.0
+OUT = 2048
 
 _sb = {
     "EW": (WIN, "bfloat16"), "LKW": (WIN, "float32"), "LKP": (8192, "float32"), "NMW": (2048, "bfloat16"),
@@ -19,18 +20,19 @@ _sb = {
     "C4": (160, "int32"), "C2": (160, "int32"), "C1": (160, "int32"), "CQ2": (160, "int32"), "CH": (128, "int32"),
     "CK": (128, "int32"), "CKT": (128, "float32"), "CKU": (128, "float32"), "KEY": (128, "int32"), "CT": (128, "int32"), "CT2": (128, "int32"),
     "CU": (128, "float32"), "CU2": (128, "float32"), "CU3": (128, "float32"), "CU4": (128, "float32"), "CU5": (128, "float32"), "CU6": (128, "float32"),
+    "CU7": (128, "float32"), "CU8": (128, "float32"), "CU9": (128, "float32"),
     "SAM2": (128, "float32"), "E1": (128, "float32"), "EQ": (128, "float32"), "GT": (128, "float32"),
     "GT1": (128, "float32"), "TC": (128, "float32"),
     "SELB": (144, "bfloat16"), "BN": (144, "float16"), "BN8": (144, "float16"),
     "BW1": (144, "bfloat16"), "BW2": (144, "bfloat16"), "BD": (576, "bfloat16"),
-    "TRIA": (128, "bfloat16"), "TRIB": (128, "bfloat16"), "TRIX": (128, "bfloat16"), "TRR": (128, "bfloat16"),
-    "IB": (128, "bfloat16"), "IM": (128, "bfloat16"), "I19": (128, "bfloat16"), "I8": (128, "bfloat16"), "IM8": (128, "bfloat16"),
-    "I256": (128, "float32"), "SHF": (128, "bfloat16"), "BO4": (128, "bfloat16"), "BO1": (128, "bfloat16"),
-    "BW1X": (128, "bfloat16"), "BW2X": (128, "bfloat16"), "RDX": (128, "bfloat16"), "QT": (128, "float32"),
+    "TRIA": (128, "bfloat16"), "TRIB": (128, "bfloat16"), "TRIX": (128, "bfloat16"), "RM": (512, "float16"), "RC": (512, "float16"),
+    "IB": (128, "bfloat16"), "IN": (128, "bfloat16"), "I19": (128, "bfloat16"), "I8": (128, "bfloat16"), "IM8": (128, "bfloat16"),
+    "I256": (128, "float32"), "SHF": (128, "bfloat16"), "BO4": (128, "bfloat16"),
+    "BW1X": (128, "bfloat16"), "BW2X": (128, "bfloat16"), "RDX": (128, "bfloat16"), "QT": (128, "float32"), "QTB": (128, "bfloat16"),
     "LO32": (128, "bfloat16"), "HI32": (128, "bfloat16"), "LO8": (128, "bfloat16"), "HI8": (128, "bfloat16"), "YDM": (32, "bfloat16"),
     "MASK": (64, "float32"), "DIAG": (64, "float32"), "QOFF": (64, "uint16"),
     "PD_": (16, "float32"), "CA": (16, "float32"), "CB": (16, "float32"), "CC": (16, "float32"), "CD": (4, "float32"),
-    "ZER": (16, "bfloat16"),
+    "ZER": (64, "bfloat16"),
     "GW": (320, "bfloat16"), "QW": (320, "int32"), "KW": (320, "int32"), "DW": (320, "bfloat16"),
     "V": (256, "int32"), "DN": (256, "bfloat16"), "DB": (256, "bfloat16"),
     "YI": (256, "int32"), "YA": (256, "int32"), "X": (256, "float16"), "QR": (256, "int32"),
@@ -42,8 +44,8 @@ _sb = {
     "LF": (16, "uint16"), "LO": (16, "uint16"), "LM": (16, "uint16"),
     "Q4": (1024, "bfloat16"), "UI": (128, "int32"), "UM": (128, "int32"), "PR": (64, "int32"), "VV": (64, "int32"), "PV": (64, "int32"),
     "SR": (256, "int32"), "SS": (256, "int32"), "OFF": (256, "uint16"), "NS": (256, "float32"),
-    "DA": (2048, "bfloat16"), "DD": (2048, "bfloat16"), "OK": (256, "bfloat16"), "MN": (256, "float32"), "AC": (256, "float32"),
-    "MS": (16, "bfloat16"), "CUM": (32, "bfloat16"), "OM": (16, "float32"), "FA": (16, "float32"), "FC": (16, "float32"),
+    "DA": (2048, "bfloat16"), "DD": (2048, "bfloat16"), "DR": (512, "bfloat16"), "OK": (256, "bfloat16"), "MN": (256, "float32"), "AC": (256, "float32"),
+    "MS": (64, "float16"), "CUM": (96, "float16"), "OM": (16, "float32"), "FA": (16, "float32"), "FC": (16, "float32"),
     "FB": (16, "float32"), "FD": (16, "float32"),
     "PKS": (256, "float32"), "CQ": (512, "int32"), "QL": (64, "int32"), "RL": (64, "int32"), "RS": (64, "int32"),
     "DQ": (64, "int32"), "DN1": (64, "int32"), "DNB": (64, "bfloat16"), "DK": (64, "int32"), "Q16": (1024, "bfloat16"),
@@ -101,7 +103,7 @@ def rank_program(g, core, T, topo):
         for k in R:
             toks += [(t, True) for t in wr.get(k, [])]
             if len(k) == 2 and k[0] == "P" and k[1] in "ABCDEFGH":
-                toks += [(t, False) for t in rd.get(k, [])]
+                toks += [(t, False) for t in rd.get(k, []) if t[4] != e]
         for k in W:
             toks += [(t, False) for t in wr.get(k, []) + rd.get(k, [])]
         toks.sort(key=lambda x: -x[0][3])
@@ -265,23 +267,31 @@ def rank_program(g, core, T, topo):
     EALL = b("EW", key=("EW.e", "EW.q", "EW.s"))
     LALL = b("LKW", key=("LKW.e", "LKW.k", "LKW.s"))
 
-    def dense(ps, n, out):
-        tt(b("TM", 0, n), ps, b("MASK", 0, n), A.mult)
+    def dense(ps, n, out, masked=False):
+        if not masked:
+            tt(b("TM", 0, n), ps, b("MASK", 0, n), A.mult)
         tt(b("A1", 0, n // 2), b("TM", 0, n, 2), b("TM", 1, n, 2), A.add)
         tt(out, b("A1", 0, n // 2, 2), b("A1", 1, n // 2, 2), A.add)
 
     def rho_sums(gs, n):
         mm(b("PA", 0, n), [(b("BO4"), gs)])
 
-    def chosen_link(ks, n, x):
+    def chosen_link(ks, n, x, mid=None, mid2=None, wanted=True):
         yi, ya, xx = b("YI" + x, 0, n), b("YA" + x, 0, n), b("X" + x, 0, n)
-        ts(yi, b("PA", 0, n), col(5), A.add)
-        ts(ya, yi, 61440, A.bitwise_and)
-        tt(xx, ya, ks, A.max)
-        mm(b("PA", 256, 256 + n // 4), [(b("BN", 3 - y, 131 - y), b("X" + x, y, n, 4)) for y in range(4)])
+        if wanted:
+            ts(yi, b("PA", 0, n), col(5), A.add)
+        if mid:
+            mid()
+        if wanted:
+            ts(ya, yi, 61440, A.bitwise_and)
+        if mid2:
+            mid2()
+        if wanted:
+            tt(xx, ya, ks, A.max)
+            mm(b("PA", 256, 256 + n // 4), [(b("BN", 3 - y, 131 - y), b("X" + x, y, n, 4)) for y in range(4)])
 
-    def wish(gs, n, x, out):
-        dense(b("PA", 256, 256 + n // 4), n // 4, b("TN2", 0, n // 16))
+    def wish(gs, n, x, out, masked=False):
+        dense(b("PA", 256, 256 + n // 4), n // 4, b("TN2", 0, n // 16), masked)
         ts(b("LST", 0, n // 16), b("TN2", 0, n // 16), -491520.0, A.add)
         tt(b("QR" + x, 0, n), ind(b("NMW"), b("LST", 0, n // 16)), gs, A.add)
         ts(out, b("QR" + x, 0, n), 255, A.bitwise_and)
@@ -328,61 +338,75 @@ def rank_program(g, core, T, topo):
     op("v", "set", b("COL", 30, 31, key="COL30"), -15.5)
     op("v", "set", b("COL", 31, 32, key="COL31"), -16.0)
 
-    def rest_of_constants():
-        ts(b("SELB"), b("RI", 0, 144), 15.0, A.is_equal)
-        ts(kt(1), b("KI"), 2, A.arith_shift_right)
+    def constants_of_the_match():
         ts(b("E1"), b("CK"), 0.0, A.is_equal)
+        ts(kt(1), b("KI"), 2, A.arith_shift_right)
+        ts(b("SELB"), b("RI", 0, 144), 15.0, A.is_equal)
+        cp(col(2), kt(1))
         ts(b("EQ"), b("CK"), 0.0, A.is_equal, SEL, A.mult)
         ts(b("GT"), b("CK"), 0.0, A.is_gt, SEL, A.mult)
-        cp(col(2), kt(1))
-        cp(col(3), kt(2))
-        cp(col(9), kt(3))
         ts(b("SAM2"), b("C2", 0, 128), col(2), A.is_equal)
-        tt(b("TC"), b("EQ"), b("GT"), A.subtract)
-        ts(b("QT"), b("KEY"), col(2), A.is_equal)
-        for nm, w in (("IB", 1.0), ("I19", 524288.0), ("I256", 256.0), ("IM", -4096.0), ("I8", 8.0), ("IM8", -8.0)):
+        for nm, w in (("I256", 256.0), ("I19", 524288.0), ("IB", 1.0), ("IN", -1.0)):
             act(b(nm), b("E1"), scale=w)
+        ts(b("QT"), b("KEY"), col(2), A.is_equal)
+        tt(b("TC"), b("EQ"), b("GT"), A.subtract)
         act(b("TRIB"), b("SAM2"), scale=-SEL)
-        for nm, w in (("BO1", 1.0), ("BW1X", w1c), ("BW2X", w2c)):
-            act(b(nm), SAME, scale=w)
-        tt(b("TRIA"), b("SAM2"), b("TC"), A.mult)
-        tt(b("TRIX"), SAME, b("TC"), A.mult)
+        act(b("QTB"), b("QT"))
         ts(b("CU5"), b("CK"), 0.0, A.is_ge)
-        tt(b("TRR"), SAME, b("CU5"), A.mult)
-        ts(b("CU4"), b("CQ2", 0, 128), col(9), A.is_equal, col(8), A.mult)
-        tt(b("RDX"), b("CU4"), SAME, A.mult)
-        ts(b("GT1"), b("CK"), 1.0, A.is_equal)
-        ts(b("CU6"), b("C1", 0, 128), 0.0, A.not_equal)
-        tt(b("SHF"), b("GT1"), b("CU6"), A.mult)
-        ts(b("DIAG"), b("CT2", 0, 64), col(3), A.is_equal)
-        cp(b("QOFF"), b("CI", 0, 64))
+        tt(b("TRIA"), b("SAM2"), b("TC"), A.mult)
+        ts(b("CU7"), b("E1"), -float(OUT), A.mult)
         ts(b("PD_"), b("PI"), col(0), A.subtract)
-        ts(b("CA"), b("PD_"), 256.0 - 4095.0, A.add)
-        ts(b("CB"), b("PD_"), 64.0 - 4095.0, A.add)
+        tt(b("CU8"), b("CU7"), b("CU5"), A.add)
+        ts(b("CA"), b("PD_"), 257.0 - OUT, A.add)
+        for z in range(4):
+            ts(col(24 + z), kt(4), float(z), A.is_equal)
+        tt(b("CU9"), b("CU8"), b("SAM2"), A.mult)
+        ts(b("CUM"), b("CI", 0, 96), 0.0, A.mult)
+        for z in range(4):
+            ts(b("RC", 128 * z, 128 * z + 128, key="RC%d" % z), b("SAM2"), col(24 + z), A.mult)
+        for z in range(4):
+            ts(b("RM", 128 * z, 128 * z + 128, key="RM%d" % z), b("CU9"), col(24 + z), A.mult)
+        op("v", "set", b("ZER"), 0.0)
+        op("v", "set", b("CQ", 0, NC), 0)
+
+    def constants_of_the_rest():
+        cp(col(9), kt(3))
+        cp(col(3), kt(2))
+        for nm, w in (("BW1X", w1c), ("BW2X", w2c)):
+            act(b(nm), SAME, scale=w)
+        ts(b("CU4"), b("CQ2", 0, 128), col(9), A.is_equal, col(8), A.mult)
+        cp(b("QOFF"), b("CI", 0, 64))
+        tt(b("RDX"), b("CU4"), SAME, A.mult)
+        tt(b("TRIX"), SAME, b("TC"), A.mult)
+        ts(b("DIAG"), b("CT2", 0, 64), col(3), A.is_equal)
+        ts(b("CB"), b("PD_"), 65.0 - OUT, A.add)
         ts(b("CC"), b("PD_"), -1.0, A.mult, SEL - KEEP, A.add)
         ts(b("CD"), b("PD_", 0, 4), -1.0, A.mult, SEL - ASK, A.add)
-        op("v", "set", b("ZER"), 0.0)
-        op("v", "set", b("CUM"), 0.0)
-        op("v", "set", b("CQ"), 0)
         op("v", "set", b("EW", ASK, WIN, key="EW.s"), 0.0)
         op("v", "set", b("LKW", ASK, WIN, key="LKW.s"), 0.0)
+        for nm, w in (("I8", 8.0), ("IM8", -8.0)):
+            act(b(nm), b("E1"), scale=w)
+        ts(b("GT1"), b("CK"), 1.0, A.is_equal)
+        ts(b("CU6"), b("C1", 0, 128), 0.0, A.not_equal)
         ts(col(14), kt(4), 0.0, A.is_equal)
         ts(col(15), kt(4), 1.0, A.is_equal, 16.0, A.mult)
         ts(col(19), col(1), 4.0, A.mult)
+        tt(b("SHF"), b("GT1"), b("CU6"), A.mult)
         tt(col(18), col(14), col(15), A.add)
         tt(col(23), col(19), col(9), A.add)
         ts(b("YDM"), b("CI", 0, 32), col(23), A.is_equal, col(18), A.mult)
 
-    def nibbles(v, n, x):
-        ts(b("ND" + x, 0, n), v, 11, A.arith_shift_right, 31, A.bitwise_and)
-        nb = b("NDB" if n == 256 else "NB6")
-        fb = b("FBS" if n == 256 else "FB6")
-        cp(nb, b("ND" + x, 0, n))
+    def nibbles(x=""):
+        nb = b("NB6" if x else "NDB")
+        fb = b("FB6" if x else "FBS")
+        cp(nb, b("ND" + x))
         act(fb, nb, F.Sign, bias=b("COL", 30, 31, key="COL30"))
         return nb, fb
 
-    def directories(nb, fb, n, dn, db, cm, out):
+    def directories(nb, fb, n, dn, db, cm, out, mid=None):
         mm(b("PH", 256, 256 + n), [(b("SHF"), dn), (b("IB"), nb), (b("I8"), fb)])
+        if mid:
+            mid()
         tt(cm, b("PH", 256, 256 + n), db, A.max)
         mm(b("PH", 0, n), [(b("IB"), cm), (b("IM8"), fb)])
         act(out, b("PH", 0, n), F.Identity, bias=b("COL", 31, 32, key="COL31"))
@@ -396,26 +420,32 @@ def rank_program(g, core, T, topo):
         for m in range(4):
             act(b("Q4", m, 1024, 4), q)
         if step == 0:
-            rest_of_constants()
+            constants_of_the_match()
         cp(b("UI"), b("PB", 0, 128))
         ts(b("UM"), b("UI"), 4095, A.bitwise_and)
         tt(b("PR"), b("UM", 0, 64), b("UM", 64, 128), A.mult)
         ts(b("VV"), b("UM", 0, 64), col(6), A.mult, col(7), A.add)
         tt(b("PV"), b("PR"), b("VV"), A.add)
+        for d in range(4):
+            tt(b("SR", 64 * d, 64 * d + 64, key="SR.%d" % d), b("PV"), b("PC", 64 * d, 64 * d + 64), A.add)
+        for h in (0, 2):
+            ts(b("SS", 64 * h, 64 * h + 128, key="SS%d" % h), b("SR", 64 * h, 64 * h + 128, key=("SR.%d" % h, "SR.%d" % (h + 1))),
+               5, A.arith_shift_right, 8191, A.bitwise_and)
+        for h in (0, 2):
+            cp(b("OFF", 64 * h, 64 * h + 128, key="OFF%d" % h), b("SS", 64 * h, 64 * h + 128, key="SS%d" % h))
 
-        def probes(d0, d1):
-            k0, k1 = 64 * d0, 64 * d1
-            for d in range(d0, d1):
-                tt(b("SR", 64 * d, 64 * d + 64, key="SR.%d" % d), b("PV"), b("PC", 64 * d, 64 * d + 64), A.add)
-            ts(b("SS", k0, k1, key="SS%d" % d0), b("SR", k0, k1, key=tuple("SR.%d" % d for d in range(d0, d1))), 5, A.arith_shift_right, 8191, A.bitwise_and)
-            cp(b("OFF", k0, k1, key="OFF%d" % d0), b("SS", k0, k1, key="SS%d" % d0))
+        def slots(d, h):
+            return ind(ENT, b("OFF", 64 * d + 32 * h, 64 * d + 32 * h + 32, key="OFF%d" % (d // 2 * 2)))
 
         def probe(d, h):
             lo = 1024 * (d % 2) + 512 * h
             k = "%d.%d" % (d % 2, h)
-            tt(b("DA", lo, lo + 512, key="DA" + k), ind(ENT, b("OFF", 64 * d + 32 * h, 64 * d + 32 * h + 32, key="OFF%d" % (1 if d else 0))),
-               b("Q4", 512 * h, 512 * h + 512), A.subtract)
-            act(b("DD", lo, lo + 512, key="DD" + k), b("DA", lo, lo + 512, key="DA" + k), F.Abs)
+            dd, dif = b("DD", lo, lo + 512, key="DD" + k), b("DA", lo, lo + 512, key="DA" + k)
+            if (d, h) == (1, 1):
+                act(dd, b("PA"), F.Abs)
+                return
+            tt(dif, slots(d, h), b("Q4", 512 * h, 512 * h + 512), A.subtract)
+            act(dd, dif, F.Abs)
 
         def distance(d):
             x = d % 2
@@ -424,23 +454,27 @@ def rank_program(g, core, T, topo):
 
         def okay(d):
             ts(b("OK", 64 * d, 64 * d + 64, key="OK%d" % d), b("PD" if d % 2 == 0 else "PE", 0, 64), th, A.is_le)
-            mm(b("PF" if d % 2 == 0 else "PG", 0, 64),
+            if d == 3:
+                mm(b("PB", 256, 320), [(b("QTB"), b("OK", 64 * e, 64 * e + 64, key="OK%d" % e)) for e in range(4)])
+            mm(b("PF" if d % 2 == 0 else "PG", 64 * d, 64 * d + 64),
                [(b("TRIB"), b("OK", 64 * e, 64 * e + 64, key="OK%d" % e)) for e in range(d)] + [(b("TRIA"), b("OK", 64 * d, 64 * d + 64, key="OK%d" % d))])
 
-        def first(d):
-            mn = b("MN", 64 * d, 64 * d + 64, key="MN%d" % d)
-            tt(mn, b("PF" if d % 2 == 0 else "PG", 0, 64), b("NS", 64 * d, 64 * d + 64, key="NS%d" % (1 if d else 0)), A.min)
-            ac = b("AC", 64 * d, 64 * d + 64, key="AC%d" % d)
+        def least(d):
+            tt(b("MN", 64 * d, 64 * d + 64, key="MN%d" % d), b("PF" if d % 2 == 0 else "PG", 64 * d, 64 * d + 64),
+               b("NS", 64 * d, 64 * d + 64, key="NS0"), A.min)
+
+        def most(d):
+            ac, mn = b("AC", 64 * d, 64 * d + 64, key="AC%d" % d), b("MN", 64 * d, 64 * d + 64, key="MN%d" % d)
             if d == 0:
                 ts(ac, mn, 0.0, A.max)
             else:
                 tt(ac, mn, b("AC", 64 * d - 64, 64 * d, key="AC%d" % (d - 1)), A.max)
 
-        probes(0, 1)
+        act(b("DR"), slots(1, 1))
         probe(0, 0)
         probe(0, 1)
-        probes(1, 4)
         mm(b("PH", 0, 256), [(b("I256"), oldk), (b("I19"), b("DN")), (b("IB"), q)])
+        mm(b("PA"), [(b("IN"), b("Q4", 512, 1024)), (b("IB"), b("DR"))])
         distance(0)
         probe(1, 0)
         probe(1, 1)
@@ -453,28 +487,34 @@ def rank_program(g, core, T, topo):
         probe(3, 0)
         okay(1)
         probe(3, 1)
-        ts(b("NS", 0, 64, key="NS0"), b("SS", 0, 64, key="SS0"), -1.0, A.mult, SEL, A.add)
-        first(0)
+        ts(b("NS", key="NS0"), b("SS", key=("SS0", "SS2")), -1.0, A.mult, SEL, A.add)
         okay(2)
-        ts(b("NS", 64, 256, key="NS1"), b("SS", 64, 256, key="SS1"), -1.0, A.mult, SEL, A.add)
         distance(3)
-        first(1)
-        first(2)
+        least(0)
+        least(1)
+        most(0)
+        least(2)
+        most(1)
+        most(2)
         okay(3)
-        first(3)
-        mm(b("PF", 64, 128), [(b("QT"), b("AC", 192, 256, key="AC3"))])
-        dense(b("PF", 64, 128), 64, b("TN"))
-        ts(b("MS"), b("TN"), 0.0, A.is_equal)
-        op("v", "scan", b("CUM", 1, 17), b("MS"), b("ZER"), 0.0, A.add, A.add)
-        mm(b("PG", 64, 80), [(b("TRR"), b("MS")), (b("IM"), b("MS")), (b("BO1"), b("CUM", 0, 16))])
-        tt(b("OM"), b("PG", 64, 80), b("CA"), A.min)
-        ts(b("LO"), b("OM"), 4095.0, A.add)
+        ts(b("MS"), b("PB", 256, 320), 0.0, A.is_equal)
+        least(3)
+        op("v", "scan", b("CUM", 1, 65), b("MS"), b("ZER"), 0.0, A.add, A.add)
+        mm(b("PD", 64, 80), [(b("RM", 128 * z, 128 * z + 128, key="RM%d" % z), b("MS", z, 64, 4)) for z in range(4)]
+           + [(b("RC", 128 * z, 128 * z + 128, key="RC%d" % z), b("CUM", z, 64, 4)) for z in range(4)])
+        most(3)
+        mm(b("PF", 256, 320), [(b("QT"), b("AC", 192, 256, key="AC3"))])
+        tt(b("OM"), b("PD", 64, 80), b("CA"), A.min)
+        tt(b("TM"), b("PF", 256, 320), b("MASK"), A.mult)
+        ts(b("LO"), b("OM"), OUT - 1.0, A.add)
         op("v", "cp", (("CQ", "LO"), b("CQ")[1].indirect(b("LO")[1])), b("PKS"), W=["CQ"])
         send(nxt, b("QL"), b("CQ", 0, NC), "qa", "ql")
+
         if step == 0:
+            constants_of_the_rest()
             for z in range(16):
                 act(b("LKW", 512 * z, 512 * z + 512, key="LKW.e"), b("LKP", z, 8192, 16, key=("LKP0", "LKP1")))
-
+        dense(None, 64, b("TN"), True)
         tt(b("FC"), b("TN"), b("CC"), A.max)
         ts(b("LF"), b("FC"), -1.0, A.mult, SEL, A.add)
 
@@ -483,10 +523,9 @@ def rank_program(g, core, T, topo):
             if not last:
                 rho_sums(Gm, 256)
             cp(b("V"), ind(LALL, b("LF")))
-            ts(Km, b("V"), 2047, A.bitwise_and)
-            if not last:
-                chosen_link(Km, 256, "")
-            return nibbles(b("V"), 256, "")
+            chosen_link(Km, 256, "", lambda: ts(Km, b("V"), 2047, A.bitwise_and),
+                        lambda: ts(b("ND"), b("V"), 11, A.arith_shift_right), not last)
+            return nibbles()
 
         if step:
             nb, fb = next_state()
@@ -494,18 +533,18 @@ def rank_program(g, core, T, topo):
         arrive("QL", "qa", prv)
         sq = b("EW", ASK, WIN, key="EW.s")
         ts(b("DQ"), b("QL"), 255, A.bitwise_and)
+        ts(b("DN1"), b("QL"), 19, A.arith_shift_right)
         cp(sq, b("DQ"))
+        cp(b("DNB"), b("DN1"))
         for h in range(2):
             act(b("Q16", 512 * h, 512 * h + 512, key="Q16%d" % h), ind(sq, b("QOFF", 32 * h, 32 * h + 32)), F.Copy)
         mm(b("PB", 128, 192), [(b("BW1X"), sq)])
         mm(b("PB", 192, 256), [(b("BW2X"), sq)])
-        ts(b("DN1"), b("QL"), 19, A.arith_shift_right)
-        cp(b("DNB"), b("DN1"))
         mm(b("PC", 0, 64), [(b("RDX"), b("DNB"))])
         cp(b("UI"), b("PB", 128, 256))
         ts(b("UM"), b("UI"), 4095, A.bitwise_and)
-        tt(b("PR"), b("UM", 0, 64), b("UM", 64, 128), A.mult)
         ts(b("VV"), b("UM", 0, 64), col(6), A.mult, col(7), A.add)
+        tt(b("PR"), b("UM", 0, 64), b("UM", 64, 128), A.mult)
         tt(b("PV"), b("VV"), b("PC", 0, 64), A.add)
         tt(b("SR", 0, 64, key="SR.0"), b("PR"), b("PV"), A.add)
         ts(b("SS", 0, 64, key="SS0"), b("SR", 0, 64, key="SR.0"), 5, A.arith_shift_right, 8191, A.bitwise_and)
@@ -515,12 +554,12 @@ def rank_program(g, core, T, topo):
             tt(sa, ind(ENT, b("OFF", 16 * c, 16 * c + 16, key="OFF0")), b("Q16", 256 * c, 256 * c + 256, key="Q16%d" % (c // 2)), A.subtract)
             act(sd, sa, F.Abs)
         ts(b("DK"), b("QL"), 8, A.arith_shift_right, 2047, A.bitwise_and)
-        cp(b("LKW", ASK, WIN, key="LKW.s"), b("DK"))
+        ts(b("FA"), b("OM"), 64.5 - OUT, A.is_gt, SEL, A.mult)
         ts(b("NS", 0, 64, key="NS0"), b("SS", 0, 64, key="SS0"), -1.0, A.mult, SEL, A.add)
-        ts(b("FA"), b("OM"), 63.5 - 4095.0, A.is_gt, SEL, A.mult)
+        cp(b("LKW", ASK, WIN, key="LKW.s"), b("DK"))
         tt(b("FD"), b("OM"), b("FA"), A.add)
         tt(b("FB"), b("FD"), b("CB"), A.min)
-        ts(b("LM"), b("FB"), 4095.0, A.add)
+        ts(b("LM"), b("FB"), OUT - 1.0, A.add)
         mm(b("PD", 0, 64), [(b("SELB", 15 - x, 143 - x), b("SD", x, 1024, 16, key=("SD0", "SD1", "SD2", "SD3"))) for x in range(16)])
         ts(b("OK", 0, 64, key="OK0"), b("PD", 0, 64), th, A.is_le)
         mm(b("PF", 0, 64), [(b("TRIX"), b("OK", 0, 64, key="OK0"))])
@@ -529,8 +568,8 @@ def rank_program(g, core, T, topo):
         mm(b("PG", 0, 64), [(SAME, b("AC", 0, 64, key="AC0"))])
         tt(b("TM"), b("PG", 0, 64), b("DIAG"), A.mult)
         for c in range(4):
-            op("v", "red", b("TS", c, c + 1), b("TM", 16 * c, 16 * c + 16), AxisListType.X, A.add)
-        tt(b("SF"), b("TS"), b("CD"), A.max)
+            op("v", "red", b("TS", c, c + 1, key="TS%d" % c), b("TM", 16 * c, 16 * c + 16), AxisListType.X, A.add)
+        tt(b("SF"), b("TS", key=("TS0", "TS1", "TS2", "TS3")), b("CD"), A.max)
         ts(b("LS"), b("SF"), -1.0, A.mult, SEL, A.add)
         ts(b("G6"), ind(EALL, b("LS")), 65536.0, A.mult)
         tt(b("RS"), ind(LALL, b("LS")), b("G6"), A.add)
@@ -550,17 +589,19 @@ def rank_program(g, core, T, topo):
         k6 = b("KW", 0, 64, key="KW0")
         ts(b("RG"), b("RL"), 16, A.arith_shift_right)
         ts(k6, b("RL"), 2047, A.bitwise_and)
+        ts(b("ND6"), b("RL"), 11, A.arith_shift_right, 31, A.bitwise_and)
         cp(g6, b("RG"))
         if not last:
             rho_sums(g6, 64)
-        nb, fb = nibbles(b("RL"), 64, "6")
+        nb, fb = nibbles("6")
         if not last:
             chosen_link(k6, 64, "6")
-        directories(nb, fb, 64, b("DNC"), b("DBC"), b("CM6"), b("DW", 0, 64, key="DW0"))
+        directories(nb, fb, 64, b("DNC"), b("DBC"), b("CM6"), b("DW", 0, 64, key="DW0"),
+                    None if last else lambda: tt(b("TM", 0, 16), b("PA", 256, 272), b("MASK", 0, 16), A.mult))
         act(b("DN"), ind(b("DW", key=("DW0", "DW1")), b("LM")))
         if not last:
             act(b("DB"), b("DN"), F.Identity, bias=8.0)
-            wish(g6, 64, "6", b("QW", 0, 64, key="QW0"))
+            wish(g6, 64, "6", b("QW", 0, 64, key="QW0"), True)
             cp(q, ind(b("QW", key=("QW0", "QW1")), b("LM")))
             cp(oldk, ind(b("KW", key=("KW0", "KW1")), b("LM")))
 

from concourse.mybir import dt, AluOpType, AxisListType, ActivationFunctionType

A = AluOpType
F = ActivationFunctionType
STEPS = 6
NC = 64
KEEP, ASK, WIN = 8192, 8448, 8512
BIGC = 23 * 262144
SEL = 16384.0
OUT = 2048

_sb = {
    "EW": (WIN, "bfloat16"), "LKW": (WIN, "float32"), "LKP": (8192, "float32"), "NMW": (2048, "bfloat16"),
    "LKI": (1024, "int32"), "LKD": (1024, "float32"), "SGI": (512, "int32"), "SGU": (512, "uint16"),
    "WTI": (2, "int32"), "THI": (1, "int32"), "S0I": (256, "int32"), "S0H": (256, "float16"),
    "DRI": (1024, "int32"), "DRT": (1024, "int32"), "DRL": (1024, "bfloat16"), "DRH": (1024, "bfloat16"),
    "D32I": (256, "int32"), "D32T": (256, "int32"), "D32L": (256, "bfloat16"), "D32H": (256, "bfloat16"), "D32U": (256, "int32"),
    "KI": (1, "int32"), "CI": (160, "int32"), "PI": (16, "int32"), "KT": (8, "int32"), "COL": (32, "float32"),
    "RI": (160, "int32"), "R2": (160, "int32"), "W1F": (160, "float32"), "W2F": (160, "float32"), "SAME": (160, "float32"),
    "C4": (160, "int32"), "C2": (160, "int32"), "C1": (160, "int32"), "CQ2": (160, "int32"), "CH": (128, "int32"),
    "CK": (128, "int32"), "CKT": (128, "float32"), "CKU": (128, "float32"), "KEY": (128, "int32"), "CT": (128, "int32"), "CT2": (128, "int32"),
    "CU": (128, "float32"), "CU2": (128, "float32"), "CU3": (128, "float32"), "CU4": (128, "float32"), "CU5": (128, "float32"), "CU6": (128, "float32"),
    "CU7": (128, "float32"), "CU8": (128, "float32"), "CU9": (128, "float32"),
    "SAM2": (128, "float32"), "E1": (128, "float32"), "EQ": (128, "float32"), "GT": (128, "float32"),
    "GT1": (128, "float32"), "TC": (128, "float32"),
    "SELB": (144, "bfloat16"), "BN": (144, "float16"), "BN8": (144, "float16"),
    "BW1": (144, "bfloat16"), "BW2": (144, "bfloat16"), "BD": (576, "bfloat16"),
    "TRIA": (128, "bfloat16"), "TRIB": (128, "bfloat16"), "TRIX": (128, "bfloat16"), "RM": (512, "float16"), "RC": (512, "float16"),
    "IB": (128, "bfloat16"), "IN": (128, "bfloat16"), "I19": (128, "bfloat16"), "I8": (128, "bfloat16"), "IM8": (128, "bfloat16"),
    "I256": (128, "float32"), "SHF": (128, "bfloat16"), "BO4": (128, "bfloat16"),
    "BW1X": (128, "bfloat16"), "BW2X": (128, "bfloat16"), "RDX": (128, "bfloat16"), "QT": (128, "float32"), "QTB": (128, "bfloat16"),
    "LO32": (128, "bfloat16"), "HI32": (128, "bfloat16"), "LO8": (128, "bfloat16"), "HI8": (128, "bfloat16"), "YDM": (32, "bfloat16"),
    "MASK": (64, "float32"), "DIAG": (64, "float32"), "QOFF": (64, "uint16"),
    "PD_": (16, "float32"), "CA": (16, "float32"), "CB": (16, "float32"), "CC": (16, "float32"), "CD": (4, "float32"),
    "ZER": (64, "bfloat16"),
    "GW": (320, "bfloat16"), "QW": (320, "int32"), "KW": (320, "int32"), "DW": (320, "bfloat16"),
    "V": (256, "int32"), "DN": (256, "bfloat16"), "DB": (256, "bfloat16"),
    "YI": (256, "int32"), "YA": (256, "int32"), "X": (256, "float16"), "QR": (256, "int32"),
    "ND": (256, "int32"), "NDB": (256, "bfloat16"), "FBS": (256, "bfloat16"), "CM": (256, "bfloat16"),
    "YI6": (64, "int32"), "YA6": (64, "int32"), "X6": (64, "float16"), "QR6": (64, "int32"),
    "ND6": (64, "int32"), "NB6": (64, "bfloat16"), "FB6": (64, "bfloat16"), "CM6": (64, "bfloat16"), "RG": (64, "int32"),
    "DC1": (64, "int32"), "DNC": (64, "bfloat16"), "DBC": (64, "bfloat16"),
    "TM": (64, "float32"), "A1": (32, "float32"), "TN": (16, "float32"), "TN2": (16, "float32"), "LST": (16, "uint16"),
    "LF": (16, "uint16"), "LO": (16, "uint16"), "LM": (16, "uint16"),
    "Q4": (1024, "bfloat16"), "UI": (128, "int32"), "UM": (128, "int32"), "PR": (64, "int32"), "VV": (64, "int32"), "PV": (64, "int32"),
    "SR": (256, "int32"), "SS": (256, "int32"), "OFF": (256, "uint16"), "NS": (256, "float32"),
    "DA": (2048, "bfloat16"), "DD": (2048, "bfloat16"), "DR": (512, "bfloat16"), "OK": (256, "bfloat16"), "MN": (256, "float32"), "AC": (256, "float32"),
    "MS": (64, "float16"), "CUM": (96, "float16"), "OM": (16, "float32"), "FA": (16, "float32"), "FC": (16, "float32"),
    "FB": (16, "float32"), "FD": (16, "float32"),
    "PKS": (256, "float32"), "CQ": (512, "int32"), "QL": (64, "int32"), "RL": (64, "int32"), "RS": (64, "int32"),
    "DQ": (64, "int32"), "DN1": (64, "int32"), "DNB": (64, "bfloat16"), "DK": (64, "int32"), "Q16": (1024, "bfloat16"),
    "SA": (1024, "bfloat16"), "SD": (1024, "bfloat16"),
    "G6": (64, "float32"), "SF": (4, "float32"), "TS": (4, "float32"), "LS": (4, "uint16"),
    "OYK": (256, "float32"), "OYG": (256, "float32"), "OYD": (256, "float32"),
}
_ALONE = {"EW", "LKW", "LKP", "NMW", "LKI", "LKD", "SGI", "SGU", "GW", "CQ", "QL", "RL", "RS", "DA", "DD", "Q4", "Q16", "QW", "KW", "DW",
          "WTI", "THI", "S0I", "DRI", "D32I", "OYK", "OYG", "OYD"}
SCRATCH = {}
PLACE = {}
_top = {}
for _n, (_w, _t) in _sb.items():
    if _n in _ALONE:
        SCRATCH["b" + _n] = ("sbuf", [128, _w], _t)
        PLACE[_n] = ("b" + _n, 0)
    else:
        _p = "pool_" + _t
        PLACE[_n] = (_p, _top.get(_p, 0))
        _top[_p] = _top.get(_p, 0) + (_w + 31) // 32 * 32
        SCRATCH[_p] = ("sbuf", [128, _top[_p]], _t)
for _n in "ABCDEFGH":
    SCRATCH["P" + _n] = ("psum", [128, 512], "float32")
LOADS = ["ls0", "ldr", "ld0", "llk", "lnm", "lwt", "lth", "lg0", "lsg", "len"]
SEMAPHORES = ["sv", "sp", "sa", "sg_", "qa", "ra", "ql", "rl", "o1", "o2", "o3"] + LOADS


def rank_program(g, core, T, topo):
    rank = T.rank_of(core)
    if rank is None:
        return
    nxt = T.cores[(rank + 1) % len(T.cores)]
    prv = T.cores[(rank - 1) % len(T.cores)]
    eng = {"v": g.vector, "p": g.tensor, "a": g.scalar, "s": g.sync, "g": g}
    own = {"v": "sv", "p": "sp", "a": "sa", "g": "sg_"}
    cnt = {s: 0 for s in SEMAPHORES}
    known = {e: {} for e in eng}
    wr, rd = {}, {}
    serial = [0]

    def b(name, lo=None, hi=None, step=1, key=None, parts=128):
        buf, at = PLACE[name] if name in PLACE else (name, 0)
        w = _sb[name][0] if name in _sb else 512
        lo = 0 if lo is None else lo
        hi = w if hi is None else hi
        last = at + lo + ((hi - lo - 1) // step) * step + 1
        keys = key if isinstance(key, tuple) else (key or name,)
        return (keys, T[buf][0:parts, at + lo:last:step] if step > 1 else T[buf][0:parts, at + lo:at + hi])

    def ind(win, off):
        return (win[0] + off[0], win[1].indirect(off[1]))

    def need(e, R, W):
        toks = []
        for k in R:
            toks += [(t, True) for t in wr.get(k, [])]
            if len(k) == 2 and k[0] == "P" and k[1] in "ABCDEFGH":
                toks += [(t, False) for t in rd.get(k, []) if t[4] != e]
        for k in W:
            toks += [(t, False) for t in wr.get(k, []) + rd.get(k, [])]
        toks.sort(key=lambda x: -x[0][3])
        for (s, n, clk, _i, te), raw in toks:
            if te == e == "p" and not raw:
                continue
            if known[e].get(s, 0) >= n:
                continue
            eng[e].wait_ge(T.sem[s], n)
            for s2, n2 in clk.items():
                if known[e].get(s2, 0) < n2:
                    known[e][s2] = n2
            known[e][s] = n

    def note(e, s, R, W, te):
        serial[0] += 1
        clk = dict(known[e])
        clk[s] = cnt[s]
        tok = (s, cnt[s], clk, serial[0], te)
        for k in R:
            rd.setdefault(k, []).append(tok)
        for k in W:
            wr[k] = [tok]
            rd[k] = []

    def split(args, R):
        out = []
        for x in args:
            if isinstance(x, tuple):
                R.extend(x[0])
                out.append(x[1])
            else:
                out.append(x)
        return out

    def op(e, meth, out, *args, sem=None, inc=1, W=None, **kw):
        R = []
        a = split(args, R)
        kv = {k: split([v], R)[0] for k, v in kw.items()}
        w = W or list(out[0])
        R.extend(k for k in out[0] if k not in w)
        need(e, R, w)
        f = {"v": {"tt": eng["v"].tensor_tensor, "ts": eng["v"].tensor_scalar, "cp": eng["v"].tensor_copy, "red": eng["v"].tensor_reduce,
                   "scan": eng["v"].tensor_tensor_scan, "set": eng["v"].memset},
             "a": {"act": eng["a"].activation, "dma": eng["a"].dma_start}, "s": {"dma": eng["s"].dma_start},
             "g": {"iota": g.iota}}[e][meth]
        s = sem or own[e]
        f(out[1], *a, **kv).then_inc(T.sem[s], inc)
        cnt[s] += inc
        note(e, s, R, w, e if sem is None else s)

    def mm(out, parts):
        R = []
        for j, x in enumerate(parts):
            r = []
            l = split(list(x), r)
            need("p", r, list(out[0]) if j == 0 else [])
            R += r
            i = eng["p"].matmul(out[1], l[0], l[1], j == 0, j == len(parts) - 1)
        i.then_inc(T.sem["sp"], 1)
        cnt["sp"] += 1
        note("p", "sp", R, list(out[0]), "p")

    def ts(out, x, s1, o1, s2=None, o2=None):
        if o2 is None:
            op("v", "ts", out, x, s1, None, o1)
        else:
            op("v", "ts", out, x, s1, s2, o1, o2)

    def tt(out, x, y, o):
        op("v", "tt", out, x, y, o)

    def cp(out, x):
        op("v", "cp", out, x)

    def act(out, x, f=F.Copy, **kw):
        op("a", "act", out, x, f, **kw)

    def load(q, sem, out, src):
        op(q, "dma", out, src, sem=sem, inc=16)

    def send(dst, land, src, rsem, lsem):
        need("g", list(src[0]), [])
        rid, pid = topo.addr(dst)[0:2]
        g.remote_dma(land[1], src[1], T.sem[rsem], T.sem[lsem], pid, rid, topo.mask(core, dst))
        cnt[lsem] += len(topo.engines(core, dst))
        note("g", lsem, list(src[0]), [], lsem)

    def arrive(key, sem, src):
        cnt[sem] += len(topo.engines(src, core))
        serial[0] += 1
        wr[key] = [(sem, cnt[sem], {sem: cnt[sem]}, serial[0], sem)]
        rd[key] = []

    def col(j):
        return b("COL", j, j + 1, key="COL%d" % j)

    def kt(j):
        return b("KT", j, j + 1, key="KT%d" % j)

    load("a", "ldr", b("DRI", parts=8), T.dr[:])
    load("s", "ls0", b("S0I", parts=8), T.s0[:])
    load("a", "llk", b("LKI"), T.lk[:])
    load("s", "lwt", b("WTI"), T.wt[:])
    load("s", "lsg", b("SGI"), T.sg[:])
    load("s", "lg0", b("GW", 64, 320, key="G"), T.g0[:])
    load("s", "ld0", b("D32I", parts=32), T.d0[:])
    load("s", "lth", b("THI"), T.th[:])
    load("s", "lnm", b("NMW"), T.nm[:])
    load("s", "len", b("EW", 0, KEEP, key="EW.e"), T.ent[:])

    for nm, pattern, down in (("KI", [[0, 1]], 1), ("C4", [[1, 10], [0, 16]], 0), ("CT", [[0, 16], [1, 8]], 0), ("C1", [[0, 40], [1, 4]], 0),
                              ("CI", [[1, 160]], 0), ("CQ2", [[0, 10], [1, 4], [0, 4]], 0), ("KEY", [[4, 8], [0, 4], [1, 4]], 0),
                              ("CK", [[1, 128]], -1), ("C2", [[1, 40], [0, 4]], 0), ("CT2", [[0, 8], [1, 16]], 0), ("PI", [[16, 16]], 1)):
        op("g", "iota", b(nm), pattern, 0, down)
    SAME = b("SAME", 0, 128)
    ts(kt(0), b("KI"), 4, A.arith_shift_right)
    ts(kt(4), b("KI"), 2, A.arith_shift_right, 3, A.bitwise_and)
    cp(col(4), b("KI"))
    ts(col(0), kt(0), 16.0, A.mult)
    cp(col(1), kt(0))
    cp(col(17), kt(4))
    ts(b("CKT"), b("C4", 0, 128), col(4), A.is_equal, 128.0, A.mult)
    ts(b("CU"), b("CT"), 0.0, A.is_equal, 16.0, A.mult)
    ts(b("CU2"), b("CT"), 4.0, A.is_equal)
    tt(b("CU3"), b("CU"), b("CU2"), A.subtract)
    tt(b("HI8"), b("CKT"), b("CU2"), A.mult)
    tt(b("LO8"), b("CKT"), b("CU3"), A.mult)
    ts(b("DRT", parts=8), b("DRI", parts=8), 15, A.bitwise_and)
    cp(b("DRH", parts=8), b("DRI", parts=8))
    cp(b("DRL", parts=8), b("DRT", parts=8))
    for h, pb in ((0, "PD"), (1, "PE")):
        mm(b(pb), [(b("HI8", parts=8), b("DRH", 512 * h, 512 * h + 512, parts=8)), (b("LO8", parts=8), b("DRL", 512 * h, 512 * h + 512, parts=8))])
    cp(b("SGU"), b("SGI"))
    for h, pb in ((0, "PD"), (1, "PE")):
        tt(b("LKD", 512 * h, 512 * h + 512), b("LKI", 512 * h, 512 * h + 512), b(pb), A.add)
    for h in range(2):
        act(b("LKP", 4096 * h, 4096 * h + 4096, key="LKP%d" % h), ind(b("LKD"), b("SGU", 256 * h, 256 * h + 256)), F.Identity, bias=32768.0)

    ts(b("W1F"), b("C4"), col(4), A.is_equal)
    ts(b("W2F"), b("C1"), 3.0, A.is_equal)
    ts(b("SAME", key="SAME"), b("C4"), col(1), A.is_equal)
    tt(b("BN8"), b("W1F", 0, 144), b("W2F", 0, 144), A.mult)
    tt(b("BN"), b("SAME", 0, 144), b("W2F", 0, 144), A.mult)
    ts(b("MASK"), b("C1", 0, 64), col(17), A.is_equal)
    cp(b("S0H", parts=8), b("S0I", parts=8))
    mm(b("PA", 256, 320), [(b("BN8", 3 - y, 131 - y, parts=8), b("S0H", y, 256, 4, parts=8)) for y in range(4)])
    ts(b("BO4"), SAME, 4096.0, A.mult)
    ts(kt(2), b("KI"), 15, A.bitwise_and)
    ts(kt(3), b("KI"), 3, A.bitwise_and)
    ts(kt(5), kt(2), -1.0, A.mult)
    ts(kt(6), kt(5), 15, A.bitwise_and)
    ts(col(5), kt(6), 4096.0, A.mult)

    Gm = b("GW", 64, 320, key="G")
    Km = b("KW", 64, 320, key="KW1")
    Qm = b("QW", 64, 320, key="QW1")
    q = b("EW", KEEP, ASK, key="EW.q")
    oldk = b("LKW", KEEP, ASK, key="LKW.k")
    ENT = b("EW", 0, KEEP, key="EW.e")
    EALL = b("EW", key=("EW.e", "EW.q", "EW.s"))
    LALL = b("LKW", key=("LKW.e", "LKW.k", "LKW.s"))

    def dense(ps, n, out, masked=False):
        if not masked:
            tt(b("TM", 0, n), ps, b("MASK", 0, n), A.mult)
        tt(b("A1", 0, n // 2), b("TM", 0, n, 2), b("TM", 1, n, 2), A.add)
        tt(out, b("A1", 0, n // 2, 2), b("A1", 1, n // 2, 2), A.add)

    def rho_sums(gs, n):
        mm(b("PA", 0, n), [(b("BO4"), gs)])

    def chosen_link(ks, n, x, mid=None, mid2=None, wanted=True):
        yi, ya, xx = b("YI" + x, 0, n), b("YA" + x, 0, n), b("X" + x, 0, n)
        if wanted:
            ts(yi, b("PA", 0, n), col(5), A.add)
        if mid:
            mid()
        if wanted:
            ts(ya, yi, 61440, A.bitwise_and)
        if mid2:
            mid2()
        if wanted:
            tt(xx, ya, ks, A.max)
            mm(b("PA", 256, 256 + n // 4), [(b("BN", 3 - y, 131 - y), b("X" + x, y, n, 4)) for y in range(4)])

    def wish(gs, n, x, out, masked=False):
        dense(b("PA", 256, 256 + n // 4), n // 4, b("TN2", 0, n // 16), masked)
        ts(b("LST", 0, n // 16), b("TN2", 0, n // 16), -491520.0, A.add)
        tt(b("QR" + x, 0, n), ind(b("NMW"), b("LST", 0, n // 16)), gs, A.add)
        ts(out, b("QR" + x, 0, n), 255, A.bitwise_and)

    dense(b("PA", 256, 320), 64, b("TN"))
    cp(b("LST"), b("TN"))
    cp(Km, ind(b("LKI"), b("LST")))
    rho_sums(Gm, 256)
    chosen_link(Km, 256, "")
    cp(oldk, Km)
    ts(b("CKU"), b("KEY"), col(4), A.is_equal)
    ts(b("CH"), b("CQ2", 0, 128), 1, A.bitwise_and)
    ts(b("CU4"), b("CH"), 0.0, A.is_equal)
    tt(b("LO32"), b("CKU"), b("CU4"), A.mult)
    tt(b("HI32"), b("CKU"), b("CH"), A.mult)
    ts(b("D32T", parts=32), b("D32I", parts=32), 15, A.bitwise_and)
    ts(b("D32U", parts=32), b("D32I", parts=32), 4, A.arith_shift_right)
    cp(b("D32L", parts=32), b("D32T", parts=32))
    cp(b("D32H", parts=32), b("D32U", parts=32))
    mm(b("PH", 0, 256), [(b("LO32", parts=32), b("D32L", parts=32)), (b("HI32", parts=32), b("D32H", parts=32))])
    wish(Gm, 256, "", Qm)
    cp(q, Qm)
    cp(b("COL", 20, 22, key="COLW"), b("WTI"))
    cp(b("COL", 22, 23, key="COL22"), b("THI"))
    th = b("COL", 22, 23, key="COL22")
    w1c, w2c = b("COL", 20, 21, key="COLW"), b("COL", 21, 22, key="COLW")
    ts(b("RI"), b("CI"), col(0), A.subtract)
    ts(b("R2"), b("RI"), 2, A.arith_shift_right)
    cp(b("DN"), b("PH", 0, 256))
    ts(b("BW1"), b("R2", 0, 144), 3.0, A.is_equal, w1c, A.mult)
    ts(b("BW2"), b("R2", 0, 144), 3.0, A.is_equal, w2c, A.mult)
    ts(col(6), kt(3), 64.0, A.mult)
    ts(col(7), kt(3), 32.0, A.mult, float(-BIGC), A.add)
    for j, w in enumerate((612.0 * 32, 9792.0 * 32, 32.0, 512.0)):
        ts(col(24 + j), kt(4), float(j), A.is_equal, w, A.mult)
    tt(col(28), col(24), col(25), A.add)
    tt(col(29), col(26), col(27), A.add)
    tt(col(8), col(28), col(29), A.add)
    for d in range(4):
        ts(col(10 + d), kt(3), float(d), A.is_equal, col(8), A.mult)
    for d in range(4):
        ts(b("BD", 144 * d, 144 * d + 144, key="BD%d" % d), b("R2", 0, 144), 3.0, A.is_equal, col(10 + d), A.mult)
    act(b("DB"), b("DN"), F.Identity, bias=8.0)
    op("v", "set", b("COL", 30, 31, key="COL30"), -15.5)
    op("v", "set", b("COL", 31, 32, key="COL31"), -16.0)

    def constants_of_the_match():
        ts(b("E1"), b("CK"), 0.0, A.is_equal)
        ts(kt(1), b("KI"), 2, A.arith_shift_right)
        ts(b("SELB"), b("RI", 0, 144), 15.0, A.is_equal)
        cp(col(2), kt(1))
        ts(b("EQ"), b("CK"), 0.0, A.is_equal, SEL, A.mult)
        ts(b("GT"), b("CK"), 0.0, A.is_gt, SEL, A.mult)
        ts(b("SAM2"), b("C2", 0, 128), col(2), A.is_equal)
        for nm, w in (("I256", 256.0), ("I19", 524288.0), ("IB", 1.0), ("IN", -1.0)):
            act(b(nm), b("E1"), scale=w)
        ts(b("QT"), b("KEY"), col(2), A.is_equal)
        tt(b("TC"), b("EQ"), b("GT"), A.subtract)
        act(b("TRIB"), b("SAM2"), scale=-SEL)
        act(b("QTB"), b("QT"))
        ts(b("CU5"), b("CK"), 0.0, A.is_ge)
        tt(b("TRIA"), b("SAM2"), b("TC"), A.mult)
        ts(b("CU7"), b("E1"), -float(OUT), A.mult)
        ts(b("PD_"), b("PI"), col(0), A.subtract)
        tt(b("CU8"), b("CU7"), b("CU5"), A.add)
        ts(b("CA"), b("PD_"), 257.0 - OUT, A.add)
        for z in range(4):
            ts(col(24 + z), kt(4), float(z), A.is_equal)
        tt(b("CU9"), b("CU8"), b("SAM2"), A.mult)
        ts(b("CUM"), b("CI", 0, 96), 0.0, A.mult)
        for z in range(4):
            ts(b("RC", 128 * z, 128 * z + 128, key="RC%d" % z), b("SAM2"), col(24 + z), A.mult)
        for z in range(4):
            ts(b("RM", 128 * z, 128 * z + 128, key="RM%d" % z), b("CU9"), col(24 + z), A.mult)
        op("v", "set", b("ZER"), 0.0)
        op("v", "set", b("CQ", 0, NC), 0)

    def constants_of_the_rest():
        cp(col(9), kt(3))
        cp(col(3), kt(2))
        for nm, w in (("BW1X", w1c), ("BW2X", w2c)):
            act(b(nm), SAME, scale=w)
        ts(b("CU4"), b("CQ2", 0, 128), col(9), A.is_equal, col(8), A.mult)
        cp(b("QOFF"), b("CI", 0, 64))
        tt(b("RDX"), b("CU4"), SAME, A.mult)
        tt(b("TRIX"), SAME, b("TC"), A.mult)
        ts(b("DIAG"), b("CT2", 0, 64), col(3), A.is_equal)
        ts(b("CB"), b("PD_"), 65.0 - OUT, A.add)
        ts(b("CC"), b("PD_"), -1.0, A.mult, SEL - KEEP, A.add)
        ts(b("CD"), b("PD_", 0, 4), -1.0, A.mult, SEL - ASK, A.add)
        op("v", "set", b("EW", ASK, WIN, key="EW.s"), 0.0)
        op("v", "set", b("LKW", ASK, WIN, key="LKW.s"), 0.0)
        for nm, w in (("I8", 8.0), ("IM8", -8.0)):
            act(b(nm), b("E1"), scale=w)
        ts(b("GT1"), b("CK"), 1.0, A.is_equal)
        ts(b("CU6"), b("C1", 0, 128), 0.0, A.not_equal)
        ts(col(14), kt(4), 0.0, A.is_equal)
        ts(col(15), kt(4), 1.0, A.is_equal, 16.0, A.mult)
        ts(col(19), col(1), 4.0, A.mult)
        tt(b("SHF"), b("GT1"), b("CU6"), A.mult)
        tt(col(18), col(14), col(15), A.add)
        tt(col(23), col(19), col(9), A.add)
        ts(b("YDM"), b("CI", 0, 32), col(23), A.is_equal, col(18), A.mult)

    def nibbles(x=""):
        nb = b("NB6" if x else "NDB")
        fb = b("FB6" if x else "FBS")
        cp(nb, b("ND" + x))
        act(fb, nb, F.Sign, bias=b("COL", 30, 31, key="COL30"))
        return nb, fb

    def directories(nb, fb, n, dn, db, cm, out, mid=None):
        mm(b("PH", 256, 256 + n), [(b("SHF"), dn), (b("IB"), nb), (b("I8"), fb)])
        if mid:
            mid()
        tt(cm, b("PH", 256, 256 + n), db, A.max)
        mm(b("PH", 0, n), [(b("IB"), cm), (b("IM8"), fb)])
        act(out, b("PH", 0, n), F.Identity, bias=b("COL", 31, 32, key="COL31"))

    for step in range(STEPS):
        last = step == STEPS - 1
        mm(b("PB", 0, 64), [(b("BW1", 12 - 4 * y, 140 - 4 * y), b("EW", KEEP + y, ASK, 4, key="EW.q")) for y in range(4)])
        mm(b("PB", 64, 128), [(b("BW2", 12 - 4 * y, 140 - 4 * y), b("EW", KEEP + y, ASK, 4, key="EW.q")) for y in range(4)])
        for d in range(4):
            mm(b("PC", 64 * d, 64 * d + 64), [(b("BD", 144 * d + 12 - 4 * y, 144 * d + 140 - 4 * y, key="BD%d" % d), b("DN", y, 256, 4)) for y in range(4)])
        for m in range(4):
            act(b("Q4", m, 1024, 4), q)
        if step == 0:
            constants_of_the_match()
        cp(b("UI"), b("PB", 0, 128))
        ts(b("UM"), b("UI"), 4095, A.bitwise_and)
        tt(b("PR"), b("UM", 0, 64), b("UM", 64, 128), A.mult)
        ts(b("VV"), b("UM", 0, 64), col(6), A.mult, col(7), A.add)
        tt(b("PV"), b("PR"), b("VV"), A.add)
        for d in range(4):
            tt(b("SR", 64 * d, 64 * d + 64, key="SR.%d" % d), b("PV"), b("PC", 64 * d, 64 * d + 64), A.add)
        for h in (0, 2):
            ts(b("SS", 64 * h, 64 * h + 128, key="SS%d" % h), b("SR", 64 * h, 64 * h + 128, key=("SR.%d" % h, "SR.%d" % (h + 1))),
               5, A.arith_shift_right, 8191, A.bitwise_and)
        for h in (0, 2):
            cp(b("OFF", 64 * h, 64 * h + 128, key="OFF%d" % h), b("SS", 64 * h, 64 * h + 128, key="SS%d" % h))

        def slots(d, h):
            return ind(ENT, b("OFF", 64 * d + 32 * h, 64 * d + 32 * h + 32, key="OFF%d" % (d // 2 * 2)))

        def probe(d, h):
            lo = 1024 * (d % 2) + 512 * h
            k = "%d.%d" % (d % 2, h)
            dd, dif = b("DD", lo, lo + 512, key="DD" + k), b("DA", lo, lo + 512, key="DA" + k)
            if (d, h) == (1, 1):
                act(dd, b("PA"), F.Abs)
                return
            tt(dif, slots(d, h), b("Q4", 512 * h, 512 * h + 512), A.subtract)
            act(dd, dif, F.Abs)

        def distance(d):
            x = d % 2
            ks = ("DD%d.0" % x, "DD%d.1" % x)
            mm(b("PD" if x == 0 else "PE", 0, 64), [(b("SELB", 15 - z, 143 - z), b("DD", 1024 * x + z, 1024 * x + 1024, 16, key=ks)) for z in range(16)])

        def okay(d):
            ts(b("OK", 64 * d, 64 * d + 64, key="OK%d" % d), b("PD" if d % 2 == 0 else "PE", 0, 64), th, A.is_le)
            if d == 3:
                mm(b("PB", 256, 320), [(b("QTB"), b("OK", 64 * e, 64 * e + 64, key="OK%d" % e)) for e in range(4)])
            mm(b("PF" if d % 2 == 0 else "PG", 64 * d, 64 * d + 64),
               [(b("TRIB"), b("OK", 64 * e, 64 * e + 64, key="OK%d" % e)) for e in range(d)] + [(b("TRIA"), b("OK", 64 * d, 64 * d + 64, key="OK%d" % d))])

        def least(d):
            tt(b("MN", 64 * d, 64 * d + 64, key="MN%d" % d), b("PF" if d % 2 == 0 else "PG", 64 * d, 64 * d + 64),
               b("NS", 64 * d, 64 * d + 64, key="NS0"), A.min)

        def most(d):
            ac, mn = b("AC", 64 * d, 64 * d + 64, key="AC%d" % d), b("MN", 64 * d, 64 * d + 64, key="MN%d" % d)
            if d == 0:
                ts(ac, mn, 0.0, A.max)
            else:
                tt(ac, mn, b("AC", 64 * d - 64, 64 * d, key="AC%d" % (d - 1)), A.max)

        act(b("DR"), slots(1, 1))
        probe(0, 0)
        probe(0, 1)
        mm(b("PH", 0, 256), [(b("I256"), oldk), (b("I19"), b("DN")), (b("IB"), q)])
        mm(b("PA"), [(b("IN"), b("Q4", 512, 1024)), (b("IB"), b("DR"))])
        distance(0)
        probe(1, 0)
        probe(1, 1)
        distance(1)
        act(b("PKS"), b("PH", 0, 256))
        probe(2, 0)
        probe(2, 1)
        okay(0)
        distance(2)
        probe(3, 0)
        okay(1)
        probe(3, 1)
        ts(b("NS", key="NS0"), b("SS", key=("SS0", "SS2")), -1.0, A.mult, SEL, A.add)
        okay(2)
        distance(3)
        least(0)
        least(1)
        most(0)
        least(2)
        most(1)
        most(2)
        okay(3)
        ts(b("MS"), b("PB", 256, 320), 0.0, A.is_equal)
        least(3)
        op("v", "scan", b("CUM", 1, 65), b("MS"), b("ZER"), 0.0, A.add, A.add)
        mm(b("PD", 64, 80), [(b("RM", 128 * z, 128 * z + 128, key="RM%d" % z), b("MS", z, 64, 4)) for z in range(4)]
           + [(b("RC", 128 * z, 128 * z + 128, key="RC%d" % z), b("CUM", z, 64, 4)) for z in range(4)])
        most(3)
        mm(b("PF", 256, 320), [(b("QT"), b("AC", 192, 256, key="AC3"))])
        tt(b("OM"), b("PD", 64, 80), b("CA"), A.min)
        tt(b("TM"), b("PF", 256, 320), b("MASK"), A.mult)
        ts(b("LO"), b("OM"), OUT - 1.0, A.add)
        op("v", "cp", (("CQ", "LO"), b("CQ")[1].indirect(b("LO")[1])), b("PKS"), W=["CQ"])
        send(nxt, b("QL"), b("CQ", 0, NC), "qa", "ql")

        if step == 0:
            constants_of_the_rest()
            for z in range(16):
                act(b("LKW", 512 * z, 512 * z + 512, key="LKW.e"), b("LKP", z, 8192, 16, key=("LKP0", "LKP1")))
        dense(None, 64, b("TN"), True)
        tt(b("FC"), b("TN"), b("CC"), A.max)
        ts(b("LF"), b("FC"), -1.0, A.mult, SEL, A.add)

        def next_state():
            act(Gm, ind(EALL, b("LF")))
            if not last:
                rho_sums(Gm, 256)
            cp(b("V"), ind(LALL, b("LF")))
            chosen_link(Km, 256, "", lambda: ts(Km, b("V"), 2047, A.bitwise_and),
                        lambda: ts(b("ND"), b("V"), 11, A.arith_shift_right), not last)
            return nibbles()

        if step:
            nb, fb = next_state()

        arrive("QL", "qa", prv)
        sq = b("EW", ASK, WIN, key="EW.s")
        ts(b("DQ"), b("QL"), 255, A.bitwise_and)
        ts(b("DN1"), b("QL"), 19, A.arith_shift_right)
        cp(sq, b("DQ"))
        cp(b("DNB"), b("DN1"))
        for h in range(2):
            act(b("Q16", 512 * h, 512 * h + 512, key="Q16%d" % h), ind(sq, b("QOFF", 32 * h, 32 * h + 32)), F.Copy)
        mm(b("PB", 128, 192), [(b("BW1X"), sq)])
        mm(b("PB", 192, 256), [(b("BW2X"), sq)])
        mm(b("PC", 0, 64), [(b("RDX"), b("DNB"))])
        cp(b("UI"), b("PB", 128, 256))
        ts(b("UM"), b("UI"), 4095, A.bitwise_and)
        ts(b("VV"), b("UM", 0, 64), col(6), A.mult, col(7), A.add)
        tt(b("PR"), b("UM", 0, 64), b("UM", 64, 128), A.mult)
        tt(b("PV"), b("VV"), b("PC", 0, 64), A.add)
        tt(b("SR", 0, 64, key="SR.0"), b("PR"), b("PV"), A.add)
        ts(b("SS", 0, 64, key="SS0"), b("SR", 0, 64, key="SR.0"), 5, A.arith_shift_right, 8191, A.bitwise_and)
        cp(b("OFF", 0, 64, key="OFF0"), b("SS", 0, 64, key="SS0"))
        for c in range(4):
            sa, sd = b("SA", 256 * c, 256 * c + 256, key="SA%d" % c), b("SD", 256 * c, 256 * c + 256, key="SD%d" % c)
            tt(sa, ind(ENT, b("OFF", 16 * c, 16 * c + 16, key="OFF0")), b("Q16", 256 * c, 256 * c + 256, key="Q16%d" % (c // 2)), A.subtract)
            act(sd, sa, F.Abs)
        ts(b("DK"), b("QL"), 8, A.arith_shift_right, 2047, A.bitwise_and)
        ts(b("FA"), b("OM"), 64.5 - OUT, A.is_gt, SEL, A.mult)
        ts(b("NS", 0, 64, key="NS0"), b("SS", 0, 64, key="SS0"), -1.0, A.mult, SEL, A.add)
        cp(b("LKW", ASK, WIN, key="LKW.s"), b("DK"))
        tt(b("FD"), b("OM"), b("FA"), A.add)
        tt(b("FB"), b("FD"), b("CB"), A.min)
        ts(b("LM"), b("FB"), OUT - 1.0, A.add)
        mm(b("PD", 0, 64), [(b("SELB", 15 - x, 143 - x), b("SD", x, 1024, 16, key=("SD0", "SD1", "SD2", "SD3"))) for x in range(16)])
        ts(b("OK", 0, 64, key="OK0"), b("PD", 0, 64), th, A.is_le)
        mm(b("PF", 0, 64), [(b("TRIX"), b("OK", 0, 64, key="OK0"))])
        tt(b("MN", 0, 64, key="MN0"), b("PF", 0, 64), b("NS", 0, 64, key="NS0"), A.min)
        ts(b("AC", 0, 64, key="AC0"), b("MN", 0, 64, key="MN0"), 0.0, A.max)
        mm(b("PG", 0, 64), [(SAME, b("AC", 0, 64, key="AC0"))])
        tt(b("TM"), b("PG", 0, 64), b("DIAG"), A.mult)
        for c in range(4):
            op("v", "red", b("TS", c, c + 1, key="TS%d" % c), b("TM", 16 * c, 16 * c + 16), AxisListType.X, A.add)
        tt(b("SF"), b("TS", key=("TS0", "TS1", "TS2", "TS3")), b("CD"), A.max)
        ts(b("LS"), b("SF"), -1.0, A.mult, SEL, A.add)
        ts(b("G6"), ind(EALL, b("LS")), 65536.0, A.mult)
        tt(b("RS"), ind(LALL, b("LS")), b("G6"), A.add)
        send(prv, b("RL"), b("RS"), "ra", "rl")

        if step == 0:
            nb, fb = next_state()
        if not last:
            wish(Gm, 256, "", Qm)
        directories(nb, fb, 256, b("DN"), b("DB"), b("CM"), b("DW", 64, 320, key="DW1"))
        ts(b("DC1"), b("CQ", 0, NC), 19, A.arith_shift_right)
        cp(b("DNC"), b("DC1"))
        ts(b("DBC"), b("DC1"), 8.0, A.add)

        arrive("RL", "ra", nxt)
        g6 = b("GW", 0, 64, key="GR")
        k6 = b("KW", 0, 64, key="KW0")
        ts(b("RG"), b("RL"), 16, A.arith_shift_right)
        ts(k6, b("RL"), 2047, A.bitwise_and)
        ts(b("ND6"), b("RL"), 11, A.arith_shift_right, 31, A.bitwise_and)
        cp(g6, b("RG"))
        if not last:
            rho_sums(g6, 64)
        nb, fb = nibbles("6")
        if not last:
            chosen_link(k6, 64, "6")
        directories(nb, fb, 64, b("DNC"), b("DBC"), b("CM6"), b("DW", 0, 64, key="DW0"),
                    None if last else lambda: tt(b("TM", 0, 16), b("PA", 256, 272), b("MASK", 0, 16), A.mult))
        act(b("DN"), ind(b("DW", key=("DW0", "DW1")), b("LM")))
        if not last:
            act(b("DB"), b("DN"), F.Identity, bias=8.0)
            wish(g6, 64, "6", b("QW", 0, 64, key="QW0"), True)
            cp(q, ind(b("QW", key=("QW0", "QW1")), b("LM")))
            cp(oldk, ind(b("KW", key=("KW0", "KW1")), b("LM")))

    cp(b("OYG"), ind(b("GW", key=("GR", "G")), b("LM")))
    op("s", "dma", (("yg",), T.yg[:]), b("OYG"), sem="o1", inc=16)
    cp(b("OYK"), ind(b("KW", key=("KW0", "KW1")), b("LM")))
    op("s", "dma", (("yk",), T.yk[:]), b("OYK"), sem="o2", inc=16)
    mm((("PA",), T.PA[0:32, 0:256]), [(b("YDM"), b("DN"))])
    cp(b("OYD", parts=32), (("PA",), T.PA[0:32, 0:256]))
    op("s", "dma", (("yd",), T.yd[:]), b("OYD", parts=32), sem="o3", inc=16)
    for s in SEMAPHORES:
        if cnt[s] > known["g"].get(s, 0):
            g.wait_ge(T.sem[s], cnt[s])
            known["g"][s] = cnt[s]
